import numpy as np
import ml_dtypes


def mxq(x, axis, fmt="e4m3"):
    dtype, down = {"e4m3": (ml_dtypes.float8_e4m3fn, 7), "e5m2": (ml_dtypes.float8_e5m2, 14)}[fmt]
    v = np.moveaxis(np.asarray(x, np.float32).astype(ml_dtypes.bfloat16).astype(np.float64), axis, -1)
    blocks = v.reshape(v.shape[:-1] + (-1, 32))
    amax = np.abs(blocks).max(-1, keepdims=True)
    byte = np.maximum(np.where(amax > 0, np.frexp(amax)[1] - 1 + 127, 0) - down, 1)
    scale = np.exp2(byte - 127.0)
    codes = (blocks / scale).astype(np.float32).astype(dtype).astype(np.float64)
    return np.moveaxis((codes * scale).reshape(v.shape), -1, axis)


WIDE = False


def mx_kscale(k):
    if not WIDE:
        return np.ones(k)
    levels = np.array([10, -10, 5, -5, 0])
    if k % 512:
        return np.exp2(np.random.permutation(np.resize(levels, k // 32))).repeat(32)
    a = np.empty((k // 512, 16))
    for p in range(k // 512):
        a[p, :8] = np.random.permutation(np.resize(levels, 8))
        for g in range(8):
            far = levels[np.abs(levels - a[p, g]) >= 10]
            a[p, g + 8] = far[np.random.randint(len(far))]
    return np.exp2(a.ravel()).repeat(32)


def f64(x):
    return np.asarray(x).astype(np.float64)


def striped(idx):
    return np.tile(idx.reshape(-1, 16).T, (8, 1)).astype(np.uint16)


def unstriped(offs):
    return offs[:16].T.reshape(-1).astype(np.int64)


def pack_weight(w):
    k, n = w.shape
    w = f64(np.asarray(w, np.float32).astype(ml_dtypes.bfloat16)).reshape(k // 32, 32, n)
    amax = np.abs(w).max(1)
    byte = np.clip(np.where(amax > 0, np.frexp(amax)[1] - 1 + 127 - 7, 1), 1, 254)
    scaled = (w * np.exp2(127.0 - byte)[:, None, :]).reshape(k, n).astype(np.float32)
    words = np.ascontiguousarray(scaled.reshape(k // 512, 128, 4, n).transpose(0, 1, 3, 2)).astype(ml_dtypes.float8_e4m3fn).view(np.uint8)
    return words, np.ascontiguousarray(byte.astype(np.uint8).reshape(k // 512, 16, n))


def unpack_weight(words, scales):
    g, p, n, _ = words.shape
    vals = np.ascontiguousarray(words).view(ml_dtypes.float8_e4m3fn).astype(np.float64) * np.repeat(np.exp2(scales.astype(np.float64) - 127.0), 8, axis=1)[..., None]
    return vals.transpose(0, 1, 3, 2).reshape(g * 512, n)


def silu(v):
    return v / (1.0 + np.exp(-np.maximum(v, -700.0)))


K, T, S, V, H, N, J, U = 512, 2048, 1024, 512, 512, 128, 512, 1024


def setup_inputs():
    n = np.random.standard_normal
    s = mx_kscale(K)[:, None]
    u = mx_kscale(H)
    r = mx_kscale(J)[:, None]
    packed_xT = pack_weight(n((K, T)) * s)
    packed_w2 = pack_weight(n((H, N)) / np.sqrt(2 * H) / u[:, None])
    return {
        "x_words": packed_xT[0],
        "x_scales": packed_xT[1],
        "aT": (n((J, U)) * r).astype(np.float32),
        "w1": (n((K, H)) / np.sqrt(K) / s * u).astype(np.float32),
        "w3": (n((J, H)) / np.sqrt(J) / r).astype(np.float32),
        "w2_words": packed_w2[0],
        "w2_scales": packed_w2[1],
        "offs": striped(np.random.permutation(T)[:S]),
        "pos1": striped(np.random.permutation(S)[:V]),
        "pos2": striped(np.random.permutation(S)[:V]),
    }


def reference(x_words, x_scales, aT, w1, w3, w2_words, w2_scales, offs, pos1, pos2):
    xq = unpack_weight(x_words, x_scales)[:, unstriped(offs)]
    h = silu(mxq(f64(w1), 0, "e4m3").T @ xq)
    f = mxq(f64(w3), 0, "e4m3").T @ mxq(f64(aT), 0, "e4m3")
    z = h[:, unstriped(pos1)] * f[:, :V] + h[:, unstriped(pos2)] * f[:, V:2 * V]
    return unpack_weight(w2_words, w2_scales).T @ mxq(z, 0, "e4m3")

@@ -1,0 +1,152 @@
+from contextlib import ExitStack
+
+import concourse.mybir as mybir
+
+F32 = mybir.dt.float32
+BF16 = mybir.dt.bfloat16
+I32 = mybir.dt.int32
+U32 = mybir.dt.uint32
+U16 = mybir.dt.uint16
+U8 = mybir.dt.uint8
+FP8X4 = mybir.dt.float8_e4m3fn_x4
+MULT = mybir.AluOpType.mult
+ADD = mybir.AluOpType.add
+SILU = mybir.ActivationFunctionType.Silu
+
+K, T, S, V, H, N, D = 512, 2048, 1024, 512, 512, 128, 2
+P = 128
+PACK = 4
+BANK = 512
+FLOPS = 2 * K * H * S + 2 * K * H * D * V + 2 * H * N * V
+
+
+def tile_picked_dime_none_p_kernel(
+    tc, x_words, x_scales, aT, w1, w3, w2_words, w2_scales, offs, pos1, pos2, out
+):
+    nc = tc.nc
+    with ExitStack() as ctx:
+        sb = ctx.enter_context(tc.tile_pool(name="sb", bufs=1))
+        psum = ctx.enter_context(tc.psum_pool(name="psum", bufs=1))
+
+        def bank(b):
+            return psum.tile([P, BANK], F32, name=f"bank{b}")
+
+        def load_scale_rows(queue, plane, rows):
+            for q in range(4):
+                queue.dma_start(plane[32 * q : 32 * q + 4, :].bitcast(I32), rows[0, 4 * q : 4 * q + 4, :].bitcast(I32))
+
+        def load_rows(name, rows):
+            raw = sb.tile([P, PACK, rows.shape[1]], F32, name=name)
+            nc.sync.dma_start(raw[:], rows.rearrange("(p j) c -> p j c", j=PACK))
+            return raw
+
+        def quantize(name, grouped, width):
+            codes = sb.tile([P, width], U32, name=name + "_codes", align_bytes=64)
+            scales = sb.tile([P, width], U8, name=name + "_scales", align_bytes=64)
+            nc.vector.quantize_mx(out=codes[:].bitcast(FP8X4), scales=scales[:], in_=grouped)
+            return codes, scales
+
+        def product(acc, stat, stat_cols, mov, mov_cols):
+            nc.tensor.matmul_mx(
+                out=acc,
+                lhsT=stat[0][:, stat_cols].bitcast(FP8X4),
+                lhsT_scale=stat[1][:, stat_cols],
+                rhs=mov[0][:, mov_cols].bitcast(FP8X4),
+                rhs_scale=mov[1][:, mov_cols],
+                start=True,
+                stop=True,
+            )
+
+        x_plane = sb.tile([P, T], U8, name="x_plane", align_bytes=64)
+        nc.vector.memset(x_plane[:].bitcast(I32), 0)
+        load_scale_rows(nc.scalar, x_plane, x_scales)
+        offs_t = sb.tile([P, S // 16], U16, name="offs_t")
+        nc.sync.dma_start(offs_t[:], offs)
+        w1_raw = load_rows("w1_raw", w1)
+        x_table = sb.tile([P, T], I32, name="x_table", align_bytes=64)
+        nc.sync.dma_start(x_table[:], x_words[0].rearrange("p n t -> p (n t)").bitcast(I32))
+        w3_raw = load_rows("w3_raw", w3)
+        pos_t = [sb.tile([P, V // 16], U16, name=f"pos{d}_t") for d in range(D)]
+        nc.sync.dma_start(pos_t[0][:], pos1)
+        a_raw = [load_rows(f"a_raw{d}", aT[:, d * V : (d + 1) * V]) for d in range(D)]
+        nc.sync.dma_start(pos_t[1][:], pos2)
+        w2_codes = sb.tile([P, N], I32, name="w2_codes", align_bytes=64)
+        nc.sync.dma_start(w2_codes[:], w2_words[0].rearrange("p n t -> p (n t)").bitcast(I32))
+        w2_plane = sb.tile([P, N], U8, name="w2_plane", align_bytes=64)
+        nc.gpsimd.memset(w2_plane[:], 0)
+        load_scale_rows(nc.sync, w2_plane, w2_scales)
+
+        picked_scales = sb.tile([P, S], U8, name="picked_scales", align_bytes=64)
+        nc.vector.tensor_copy(picked_scales[:], x_plane[:].indirect(offs_t[:]))
+
+        def deal_weight(name, raw):
+            grouped = sb.tile([P, H * PACK], BF16, name=name + "_bf16", align_bytes=64)
+            nc.vector.tensor_copy(
+                out=grouped[:].rearrange("p (t m j) -> p m j t", t=PACK, j=PACK),
+                in_=raw[:].rearrange("p j (m t) -> p m j t", t=PACK),
+            )
+            return quantize(name, grouped[:], H)
+
+        w1_q = deal_weight("w1", w1_raw)
+
+        h = [sb.tile([P, S], F32, name=f"h{t}") for t in range(PACK)]
+        pre = {}
+        for half in range(S // BANK):
+            words = sb.tile([P, BANK], U32, name=f"picked_words{half}", align_bytes=64)
+            nc.vector.tensor_copy(
+                words[:], x_table[:].bitcast(U32).indirect(offs_t[:, half * (BANK // 16) : (half + 1) * (BANK // 16)])
+            )
+            for t in range(PACK):
+                acc = bank(2 * t + half)
+                nc.tensor.matmul_mx(
+                    out=acc[:],
+                    lhsT=w1_q[0][:, t * P : (t + 1) * P].bitcast(FP8X4),
+                    lhsT_scale=w1_q[1][:, t * P : (t + 1) * P],
+                    rhs=words[:].bitcast(FP8X4),
+                    rhs_scale=picked_scales[:, half * BANK : (half + 1) * BANK],
+                    start=True,
+                    stop=True,
+                )
+                pre[t, half] = acc
+        w3_q = deal_weight("w3", w3_raw)
+        for t, half in ((0, 0), (1, 0), (0, 1), (1, 1), (2, 0), (2, 1), (3, 0), (3, 1)):
+            nc.scalar.activation(h[t][:, half * BANK : (half + 1) * BANK], pre[t, half][:], SILU)
+
+        terms = []
+        for d in range(D):
+            fetched = sb.tile([P, PACK, V], F32, name=f"fetched{d}")
+            for t in range(PACK):
+                nc.vector.tensor_copy(fetched[:, t, :], h[t][:].indirect(pos_t[d][:]))
+            grouped = sb.tile([P, V, PACK], BF16, name=f"a_bf16_{d}", align_bytes=64)
+            nc.scalar.copy(
+                out=grouped[:].rearrange("p (c i) j -> p c j i", i=4),
+                in_=a_raw[d][:].rearrange("p j (c i) -> p c j i", i=4),
+            )
+            a_q = quantize(f"a{d}", grouped[:].rearrange("p v j -> p (v j)"), V)
+            terms.append((fetched, a_q))
+        prods = []
+        for d in range(D):
+            fetched, a_q = terms[d]
+            prod = sb.tile([P, PACK, V], F32, name=f"prod{d}")
+            for t in range(PACK):
+                acc = bank(2 * t + d)
+                product(acc[:], w3_q, slice(t * P, (t + 1) * P), a_q, slice(0, V))
+                nc.vector.tensor_tensor(prod[:, t, :], fetched[:, t, :], acc[:], MULT)
+            prods.append(prod)
+
+        HALF = V // 2
+        for part in range(2):
+            cols = slice(part * HALF, (part + 1) * HALF)
+            z = sb.tile([P, HALF, PACK], BF16, name=f"z{part}", align_bytes=64)
+            nc.vector.tensor_tensor(
+                z[:].rearrange("p (c i) t -> p c t i", i=4),
+                prods[0][:, :, cols].rearrange("p t (c i) -> p c t i", i=4),
+                prods[1][:, :, cols].rearrange("p t (c i) -> p c t i", i=4),
+                ADD,
+            )
+            z_q = quantize(f"z{part}", z[:].rearrange("p v t -> p (v t)"), HALF)
+            acc = bank(part)
+            product(acc[:, 0:HALF], (w2_codes, w2_plane), slice(0, N), z_q, slice(0, HALF))
+            result = sb.tile([P, HALF], F32, name=f"result{part}")
+            nc.scalar.copy(result[:], acc[:, 0:HALF])
+            nc.sync.dma_start(out[:, cols], result[:])

@@ -18,6 +18,7 @@ P = 128
 PACK = 4
 BANK = 512
 FLOPS = 2 * K * H * S + 2 * K * H * D * V + 2 * H * N * V
+COPY = mybir.ActivationFunctionType.Copy
 
 
 def tile_picked_dime_none_p_kernel(
@@ -58,18 +59,18 @@ def tile_picked_dime_none_p_kernel(
             )
 
         x_plane = sb.tile([P, T], U8, name="x_plane", align_bytes=64)
-        nc.vector.memset(x_plane[:].bitcast(I32), 0)
-        load_scale_rows(nc.scalar, x_plane, x_scales)
+        nc.gpsimd.memset(x_plane[:].bitcast(I32), 0)
         offs_t = sb.tile([P, S // 16], U16, name="offs_t")
         nc.sync.dma_start(offs_t[:], offs)
-        w1_raw = load_rows("w1_raw", w1)
-        x_table = sb.tile([P, T], I32, name="x_table", align_bytes=64)
-        nc.sync.dma_start(x_table[:], x_words[0].rearrange("p n t -> p (n t)").bitcast(I32))
-        w3_raw = load_rows("w3_raw", w3)
         pos_t = [sb.tile([P, V // 16], U16, name=f"pos{d}_t") for d in range(D)]
         nc.sync.dma_start(pos_t[0][:], pos1)
-        a_raw = [load_rows(f"a_raw{d}", aT[:, d * V : (d + 1) * V]) for d in range(D)]
         nc.sync.dma_start(pos_t[1][:], pos2)
+        load_scale_rows(nc.sync, x_plane, x_scales)
+        x_table = sb.tile([P, T], I32, name="x_table", align_bytes=64)
+        nc.sync.dma_start(x_table[:], x_words[0].rearrange("p n t -> p (n t)").bitcast(I32))
+        w1_raw = load_rows("w1_raw", w1)
+        w3_raw = load_rows("w3_raw", w3)
+        a_raw = [load_rows(f"a_raw{d}", aT[:, d * V : (d + 1) * V]) for d in range(D)]
         w2_codes = sb.tile([P, N], I32, name="w2_codes", align_bytes=64)
         nc.sync.dma_start(w2_codes[:], w2_words[0].rearrange("p n t -> p (n t)").bitcast(I32))
         w2_plane = sb.tile([P, N], U8, name="w2_plane", align_bytes=64)
@@ -79,74 +80,92 @@ def tile_picked_dime_none_p_kernel(
         picked_scales = sb.tile([P, S], U8, name="picked_scales", align_bytes=64)
         nc.vector.tensor_copy(picked_scales[:], x_plane[:].indirect(offs_t[:]))
 
-        def deal_weight(name, raw):
-            grouped = sb.tile([P, H * PACK], BF16, name=name + "_bf16", align_bytes=64)
-            nc.vector.tensor_copy(
-                out=grouped[:].rearrange("p (t m j) -> p m j t", t=PACK, j=PACK),
-                in_=raw[:].rearrange("p j (m t) -> p m j t", t=PACK),
+        def deal_weight(name, raw, copy, t0, tiles):
+            grouped = sb.tile([P, tiles * P * PACK], BF16, name=name + "_bf16", align_bytes=64)
+            copy(
+                out=grouped[:].rearrange("p (t m j) -> p m j t", t=tiles, j=PACK),
+                in_=raw[:].rearrange("p j (m t) -> p m j t", t=PACK)[:, :, :, t0 : t0 + tiles],
             )
-            return quantize(name, grouped[:], H)
+            return grouped
 
-        w1_q = deal_weight("w1", w1_raw)
+        words = []
+        for half in range(S // BANK):
+            picked = sb.tile([P, BANK], U32, name=f"picked_words{half}", align_bytes=64)
+            nc.vector.tensor_copy(
+                picked[:], x_table[:].bitcast(U32).indirect(offs_t[:, half * (BANK // 16) : (half + 1) * (BANK // 16)])
+            )
+            words.append(picked)
+        w1_low = deal_weight("w1_low", w1_raw, nc.scalar.copy, 0, 2)
+        w1_high = deal_weight("w1_high", w1_raw, nc.vector.tensor_copy, 2, 2)
+        w1_q = [quantize("w1_low", w1_low[:], 2 * P), quantize("w1_high", w1_high[:], 2 * P)]
 
         h = [sb.tile([P, S], F32, name=f"h{t}") for t in range(PACK)]
         pre = {}
-        for half in range(S // BANK):
-            words = sb.tile([P, BANK], U32, name=f"picked_words{half}", align_bytes=64)
-            nc.vector.tensor_copy(
-                words[:], x_table[:].bitcast(U32).indirect(offs_t[:, half * (BANK // 16) : (half + 1) * (BANK // 16)])
-            )
-            for t in range(PACK):
+        for t in range(PACK):
+            codes, scales = w1_q[t // 2]
+            cols = slice(t % 2 * P, (t % 2 + 1) * P)
+            for half in range(S // BANK):
                 acc = bank(2 * t + half)
                 nc.tensor.matmul_mx(
                     out=acc[:],
-                    lhsT=w1_q[0][:, t * P : (t + 1) * P].bitcast(FP8X4),
-                    lhsT_scale=w1_q[1][:, t * P : (t + 1) * P],
-                    rhs=words[:].bitcast(FP8X4),
+                    lhsT=codes[:, cols].bitcast(FP8X4),
+                    lhsT_scale=scales[:, cols],
+                    rhs=words[half][:].bitcast(FP8X4),
                     rhs_scale=picked_scales[:, half * BANK : (half + 1) * BANK],
                     start=True,
                     stop=True,
                 )
                 pre[t, half] = acc
-        w3_q = deal_weight("w3", w3_raw)
-        for t, half in ((0, 0), (1, 0), (0, 1), (1, 1), (2, 0), (2, 1), (3, 0), (3, 1)):
+        w3_q = quantize("w3", deal_weight("w3", w3_raw, nc.vector.tensor_copy, 0, PACK)[:], H)
+        for t, half in sorted(pre):
             nc.scalar.activation(h[t][:, half * BANK : (half + 1) * BANK], pre[t, half][:], SILU)
 
-        terms = []
+        a_q = []
         for d in range(D):
-            fetched = sb.tile([P, PACK, V], F32, name=f"fetched{d}")
-            for t in range(PACK):
-                nc.vector.tensor_copy(fetched[:, t, :], h[t][:].indirect(pos_t[d][:]))
-            grouped = sb.tile([P, V, PACK], BF16, name=f"a_bf16_{d}", align_bytes=64)
-            nc.scalar.copy(
-                out=grouped[:].rearrange("p (c i) j -> p c j i", i=4),
-                in_=a_raw[d][:].rearrange("p j (c i) -> p c j i", i=4),
-            )
-            a_q = quantize(f"a{d}", grouped[:].rearrange("p v j -> p (v j)"), V)
-            terms.append((fetched, a_q))
-        prods = []
+            grouped = sb.tile([P, V, PACK], BF16, name=f"a_bf16_{d}", tag=f"shared{d}", align_bytes=64)
+            dst = grouped[:].rearrange("p (c i) j -> p c j i", i=4)
+            src = a_raw[d][:].rearrange("p j (c i) -> p c j i", i=4)
+            if d == 0 and False:
+                nc.gpsimd.tensor_scalar(dst, src, 1.0, 0.0, MULT, ADD)
+            else:
+                nc.scalar.copy(out=dst, in_=src)
+            a_q.append(quantize(f"a{d}", grouped[:].rearrange("p v j -> p (v j)"), V))
+        prods = [sb.tile([P, PACK, V], F32, name=f"prod{d}") for d in range(D)]
+        plain = ((0, 0), (1, 0), (0, 1), (1, 1), (0, 2), (0, 3))
+        fetched = {}
+        for d, t in plain:
+            tag = {(0, 3): "shared0"}.get((d, t), f"fetched{d}{t}")
+            fetched[d, t] = sb.tile([P, V], F32, name=f"fetched{d}{t}", tag=tag, align_bytes=64)
+            nc.vector.tensor_copy(fetched[d, t][:], h[t][:].indirect(pos_t[d][:]))
         for d in range(D):
-            fetched, a_q = terms[d]
-            prod = sb.tile([P, PACK, V], F32, name=f"prod{d}")
             for t in range(PACK):
                 acc = bank(2 * t + d)
-                product(acc[:], w3_q, slice(t * P, (t + 1) * P), a_q, slice(0, V))
-                nc.vector.tensor_tensor(prod[:, t, :], fetched[:, t, :], acc[:], MULT)
-            prods.append(prod)
+                product(acc[:], w3_q, slice(t * P, (t + 1) * P), a_q[d], slice(0, V))
+                if (d, t) in ():
+                    filt = sb.tile([P, V], F32, name=f"filt{d}{t}")
+                    nc.scalar.copy(filt[:], acc[:])
+                    nc.gpsimd.tensor_tensor(prods[d][:, t, :], fetched[d, t][:], filt[:], MULT)
+                elif (d, t) in plain:
+                    nc.vector.tensor_tensor(prods[d][:, t, :], fetched[d, t][:], acc[:], MULT)
+                else:
+                    filt = sb.tile([P, V], F32, name=f"filt{d}{t}")
+                    nc.scalar.copy(filt[:], acc[:])
+                    nc.vector.tensor_tensor(prods[d][:, t, :], h[t][:].indirect(pos_t[d][:]), filt[:], MULT)
 
-        HALF = V // 2
-        for part in range(2):
-            cols = slice(part * HALF, (part + 1) * HALF)
-            z = sb.tile([P, HALF, PACK], BF16, name=f"z{part}", align_bytes=64)
+        lo = 0
+        for part, width in enumerate((256, 128, 128)):
+            cols = slice(lo, lo + width)
+            lo = lo + width
+            z = sb.tile([P, width, PACK], BF16, name=f"z{part}", align_bytes=64)
             nc.vector.tensor_tensor(
                 z[:].rearrange("p (c i) t -> p c t i", i=4),
                 prods[0][:, :, cols].rearrange("p t (c i) -> p c t i", i=4),
                 prods[1][:, :, cols].rearrange("p t (c i) -> p c t i", i=4),
                 ADD,
             )
-            z_q = quantize(f"z{part}", z[:].rearrange("p v t -> p (v t)"), HALF)
+            z_q = quantize(f"z{part}", z[:].rearrange("p v t -> p (v t)"), width)
             acc = bank(part)
-            product(acc[:, 0:HALF], (w2_codes, w2_plane), slice(0, N), z_q, slice(0, HALF))
-            result = sb.tile([P, HALF], F32, name=f"result{part}")
-            nc.scalar.copy(result[:], acc[:, 0:HALF])
+            product(acc[:, 0:width], (w2_codes, w2_plane), slice(0, N), z_q, slice(0, width))
+            result = sb.tile([P, width], F32, name=f"result{part}")
+            nc.scalar.copy(result[:], acc[:, 0:width])
             nc.sync.dma_start(out[:, cols], result[:])

@@ -59,17 +59,23 @@ def tile_picked_dime_none_p_kernel(
             )
 
         x_plane = sb.tile([P, T], U8, name="x_plane", align_bytes=64)
-        nc.gpsimd.memset(x_plane[:].bitcast(I32), 0)
+        nc.gpsimd.memset(x_plane[:, : T // 2].bitcast(I32), 0)
+        nc.vector.memset(x_plane[:, T // 2 :].bitcast(I32), 0)
+        warm = sb.tile([P, 2], F32, name="warm")
+        nc.vector.memset(warm[:, 0:1], 0.0)
+        nc.scalar.activation(warm[:, 1:2], warm[:, 0:1], SILU)
         offs_t = sb.tile([P, S // 16], U16, name="offs_t")
         nc.sync.dma_start(offs_t[:], offs)
+        x_table = sb.tile([P, T], I32, name="x_table", align_bytes=64)
+        x_src = x_words[0].rearrange("p n t -> p (n t)").bitcast(I32)
+        nc.sync.dma_start(x_table[:, : T // 2], x_src[:, : T // 2])
+        load_scale_rows(nc.sync, x_plane, x_scales)
+        nc.sync.dma_start(x_table[:, T // 2 :], x_src[:, T // 2 :])
+        w1_raw = load_rows("w1_raw", w1)
+        w3_raw = load_rows("w3_raw", w3)
         pos_t = [sb.tile([P, V // 16], U16, name=f"pos{d}_t") for d in range(D)]
         nc.sync.dma_start(pos_t[0][:], pos1)
         nc.sync.dma_start(pos_t[1][:], pos2)
-        load_scale_rows(nc.sync, x_plane, x_scales)
-        x_table = sb.tile([P, T], I32, name="x_table", align_bytes=64)
-        nc.sync.dma_start(x_table[:], x_words[0].rearrange("p n t -> p (n t)").bitcast(I32))
-        w1_raw = load_rows("w1_raw", w1)
-        w3_raw = load_rows("w3_raw", w3)
         a_raw = [load_rows(f"a_raw{d}", aT[:, d * V : (d + 1) * V]) for d in range(D)]
         w2_codes = sb.tile([P, N], I32, name="w2_codes", align_bytes=64)
         nc.sync.dma_start(w2_codes[:], w2_words[0].rearrange("p n t -> p (n t)").bitcast(I32))
@@ -96,7 +102,7 @@ def tile_picked_dime_none_p_kernel(
             )
             words.append(picked)
         w1_low = deal_weight("w1_low", w1_raw, nc.scalar.copy, 0, 2)
-        w1_high = deal_weight("w1_high", w1_raw, nc.vector.tensor_copy, 2, 2)
+        w1_high = deal_weight("w1_high", w1_raw, nc.scalar.copy, 2, 2)
         w1_q = [quantize("w1_low", w1_low[:], 2 * P), quantize("w1_high", w1_high[:], 2 * P)]
 
         h = [sb.tile([P, S], F32, name=f"h{t}") for t in range(PACK)]
@@ -131,26 +137,24 @@ def tile_picked_dime_none_p_kernel(
                 nc.scalar.copy(out=dst, in_=src)
             a_q.append(quantize(f"a{d}", grouped[:].rearrange("p v j -> p (v j)"), V))
         prods = [sb.tile([P, PACK, V], F32, name=f"prod{d}") for d in range(D)]
-        plain = ((0, 0), (1, 0), (0, 1), (1, 1), (0, 2), (0, 3))
         fetched = {}
-        for d, t in plain:
-            tag = {(0, 3): "shared0"}.get((d, t), f"fetched{d}{t}")
-            fetched[d, t] = sb.tile([P, V], F32, name=f"fetched{d}{t}", tag=tag, align_bytes=64)
-            nc.vector.tensor_copy(fetched[d, t][:], h[t][:].indirect(pos_t[d][:]))
+        for d in range(D):
+            for t in range(PACK):
+                if t % 2 == 0:
+                    tag = f"shared{t // 2}" if d == 1 else f"fetched{t}"
+                    pair = sb.tile([P, 2, V], F32, name=f"fetched{d}{t}", tag=tag, align_bytes=64)
+                fetched[d, t] = pair[:, t % 2, :]
+                nc.vector.tensor_copy(fetched[d, t], h[t][:].indirect(pos_t[d][:]))
         for d in range(D):
             for t in range(PACK):
                 acc = bank(2 * t + d)
                 product(acc[:], w3_q, slice(t * P, (t + 1) * P), a_q[d], slice(0, V))
-                if (d, t) in ():
+                if d == 0:
                     filt = sb.tile([P, V], F32, name=f"filt{d}{t}")
                     nc.scalar.copy(filt[:], acc[:])
-                    nc.gpsimd.tensor_tensor(prods[d][:, t, :], fetched[d, t][:], filt[:], MULT)
-                elif (d, t) in plain:
-                    nc.vector.tensor_tensor(prods[d][:, t, :], fetched[d, t][:], acc[:], MULT)
+                    nc.gpsimd.tensor_tensor(prods[d][:, t, :], fetched[d, t], filt[:], MULT)
                 else:
-                    filt = sb.tile([P, V], F32, name=f"filt{d}{t}")
-                    nc.scalar.copy(filt[:], acc[:])
-                    nc.vector.tensor_tensor(prods[d][:, t, :], h[t][:].indirect(pos_t[d][:]), filt[:], MULT)
+                    nc.vector.tensor_tensor(prods[d][:, t, :], fetched[d, t], acc[:], MULT)
 
         lo = 0
         for part, width in enumerate((256, 128, 128)):
@@ -168,4 +172,4 @@ def tile_picked_dime_none_p_kernel(
             product(acc[:, 0:width], (w2_codes, w2_plane), slice(0, N), z_q, slice(0, width))
             result = sb.tile([P, width], F32, name=f"result{part}")
             nc.scalar.copy(result[:], acc[:, 0:width])
-            nc.sync.dma_start(out[:, cols], result[:])
+            nc.scalar.dma_start(out[:, cols], result[:])

@@ -18,7 +18,6 @@ P = 128
 PACK = 4
 BANK = 512
 FLOPS = 2 * K * H * S + 2 * K * H * D * V + 2 * H * N * V
-COPY = mybir.ActivationFunctionType.Copy
 
 
 def tile_picked_dime_none_p_kernel(
@@ -32,9 +31,10 @@ def tile_picked_dime_none_p_kernel(
         def bank(b):
             return psum.tile([P, BANK], F32, name=f"bank{b}")
 
-        def load_scale_rows(queue, plane, rows):
-            for q in range(4):
-                queue.dma_start(plane[32 * q : 32 * q + 4, :].bitcast(I32), rows[0, 4 * q : 4 * q + 4, :].bitcast(I32))
+        def load_scale_rows(plane, rows):
+            by_quadrant = rows[0].bitcast(I32).rearrange("(q r) c -> r q c", r=4)
+            for r in range(4):
+                nc.sync.dma_start(plane[r:P:32, :].bitcast(I32), by_quadrant[r])
 
         def load_rows(name, rows):
             raw = sb.tile([P, PACK, rows.shape[1]], F32, name=name)
@@ -58,9 +58,17 @@ def tile_picked_dime_none_p_kernel(
                 stop=True,
             )
 
+        def deal_weight(name, raw, copy, t0, tiles, tag=None):
+            grouped = sb.tile([P, tiles * P * PACK], BF16, name=name + "_bf16", tag=tag or name + "_bf16", align_bytes=64)
+            copy(
+                out=grouped[:].rearrange("p (t m j) -> p m j t", t=tiles, j=PACK),
+                in_=raw[:].rearrange("p j (m t) -> p m j t", t=PACK)[:, :, :, t0 : t0 + tiles],
+            )
+            return grouped
+        late = ctx.enter_context(tc.tile_pool(name="late", bufs=1))
+
         x_plane = sb.tile([P, T], U8, name="x_plane", align_bytes=64)
-        nc.gpsimd.memset(x_plane[:, : T // 2].bitcast(I32), 0)
-        nc.vector.memset(x_plane[:, T // 2 :].bitcast(I32), 0)
+        nc.gpsimd.memset(x_plane[:].bitcast(I32), 0)
         warm = sb.tile([P, 2], F32, name="warm")
         nc.vector.memset(warm[:, 0:1], 0.0)
         nc.scalar.activation(warm[:, 1:2], warm[:, 0:1], SILU)
@@ -68,9 +76,9 @@ def tile_picked_dime_none_p_kernel(
         nc.sync.dma_start(offs_t[:], offs)
         x_table = sb.tile([P, T], I32, name="x_table", align_bytes=64)
         x_src = x_words[0].rearrange("p n t -> p (n t)").bitcast(I32)
-        nc.sync.dma_start(x_table[:, : T // 2], x_src[:, : T // 2])
-        load_scale_rows(nc.sync, x_plane, x_scales)
-        nc.sync.dma_start(x_table[:, T // 2 :], x_src[:, T // 2 :])
+        nc.sync.dma_start(x_table[:, : T // 4], x_src[:, : T // 4])
+        load_scale_rows(x_plane, x_scales)
+        nc.sync.dma_start(x_table[:, T // 4 :], x_src[:, T // 4 :])
         w1_raw = load_rows("w1_raw", w1)
         w3_raw = load_rows("w3_raw", w3)
         pos_t = [sb.tile([P, V // 16], U16, name=f"pos{d}_t") for d in range(D)]
@@ -81,19 +89,10 @@ def tile_picked_dime_none_p_kernel(
         nc.sync.dma_start(w2_codes[:], w2_words[0].rearrange("p n t -> p (n t)").bitcast(I32))
         w2_plane = sb.tile([P, N], U8, name="w2_plane", align_bytes=64)
         nc.gpsimd.memset(w2_plane[:], 0)
-        load_scale_rows(nc.sync, w2_plane, w2_scales)
+        load_scale_rows(w2_plane, w2_scales)
 
         picked_scales = sb.tile([P, S], U8, name="picked_scales", align_bytes=64)
         nc.vector.tensor_copy(picked_scales[:], x_plane[:].indirect(offs_t[:]))
-
-        def deal_weight(name, raw, copy, t0, tiles):
-            grouped = sb.tile([P, tiles * P * PACK], BF16, name=name + "_bf16", align_bytes=64)
-            copy(
-                out=grouped[:].rearrange("p (t m j) -> p m j t", t=tiles, j=PACK),
-                in_=raw[:].rearrange("p j (m t) -> p m j t", t=PACK)[:, :, :, t0 : t0 + tiles],
-            )
-            return grouped
-
         words = []
         for half in range(S // BANK):
             picked = sb.tile([P, BANK], U32, name=f"picked_words{half}", align_bytes=64)
@@ -101,15 +100,19 @@ def tile_picked_dime_none_p_kernel(
                 picked[:], x_table[:].bitcast(U32).indirect(offs_t[:, half * (BANK // 16) : (half + 1) * (BANK // 16)])
             )
             words.append(picked)
-        w1_low = deal_weight("w1_low", w1_raw, nc.scalar.copy, 0, 2)
-        w1_high = deal_weight("w1_high", w1_raw, nc.scalar.copy, 2, 2)
-        w1_q = [quantize("w1_low", w1_low[:], 2 * P), quantize("w1_high", w1_high[:], 2 * P)]
+
+        w1_t0 = deal_weight("w1_t0", w1_raw, nc.scalar.copy, 0, 1, "w1_stage")
+        w1_t1 = deal_weight("w1_t1", w1_raw, nc.scalar.copy, 1, 1)
+        w1_q0 = quantize("w1_t0", w1_t0[:], P)
+        w1_high = deal_weight("w1_high", w1_raw, nc.vector.tensor_copy, 2, 2, "w1_stage")
+        w1_q1 = quantize("w1_t1", w1_t1[:], P)
+        w1_qh = quantize("w1_high", w1_high[:], 2 * P)
+        stat = [(w1_q0, 0), (w1_q1, 0), (w1_qh, 0), (w1_qh, P)]
 
         h = [sb.tile([P, S], F32, name=f"h{t}") for t in range(PACK)]
-        pre = {}
         for t in range(PACK):
-            codes, scales = w1_q[t // 2]
-            cols = slice(t % 2 * P, (t % 2 + 1) * P)
+            (codes, scales), c0 = stat[t]
+            cols = slice(c0, c0 + P)
             for half in range(S // BANK):
                 acc = bank(2 * t + half)
                 nc.tensor.matmul_mx(
@@ -121,35 +124,38 @@ def tile_picked_dime_none_p_kernel(
                     start=True,
                     stop=True,
                 )
-                pre[t, half] = acc
+                nc.scalar.activation(h[t][:, half * BANK : (half + 1) * BANK], acc[:], SILU)
         w3_q = quantize("w3", deal_weight("w3", w3_raw, nc.vector.tensor_copy, 0, PACK)[:], H)
-        for t, half in sorted(pre):
-            nc.scalar.activation(h[t][:, half * BANK : (half + 1) * BANK], pre[t, half][:], SILU)
 
         a_q = []
         for d in range(D):
-            grouped = sb.tile([P, V, PACK], BF16, name=f"a_bf16_{d}", tag=f"shared{d}", align_bytes=64)
-            dst = grouped[:].rearrange("p (c i) j -> p c j i", i=4)
-            src = a_raw[d][:].rearrange("p j (c i) -> p c j i", i=4)
-            if d == 0 and False:
-                nc.gpsimd.tensor_scalar(dst, src, 1.0, 0.0, MULT, ADD)
+            if d == 0:
+                grouped = sb.tile([P, V, PACK], BF16, name="a_bf16_0", tag="a0_stage", align_bytes=64)
+                nc.gpsimd.tensor_scalar(grouped[:], a_raw[d][:].rearrange("p j v -> p v j"), 1.0, 0.0, MULT, ADD)
             else:
-                nc.scalar.copy(out=dst, in_=src)
+                grouped = late.tile([P, V, PACK], BF16, name="a_bf16_1", offset=6144, align_bytes=64)
+                nc.scalar.copy(
+                    out=grouped[:].rearrange("p (c i) j -> p c j i", i=4),
+                    in_=a_raw[d][:].rearrange("p j (c i) -> p c j i", i=4),
+                )
             a_q.append(quantize(f"a{d}", grouped[:].rearrange("p v j -> p (v j)"), V))
-        prods = [sb.tile([P, PACK, V], F32, name=f"prod{d}") for d in range(D)]
+        prods = [
+            late.tile([P, PACK, V], F32, name="prod0", offset=8192, align_bytes=64),
+            sb.tile([P, PACK, V], F32, name="prod1"),
+        ]
+        first = sb.tile([P, 2, V], F32, name="fetched_first", align_bytes=64)
+        second = sb.tile([P, 2, V], F32, name="fetched_second", tag="a0_stage", align_bytes=64)
+        third = late.tile([P, PACK, V], F32, name="fetched_third", offset=0, align_bytes=64)
         fetched = {}
         for d in range(D):
             for t in range(PACK):
-                if t % 2 == 0:
-                    tag = f"shared{t // 2}" if d == 1 else f"fetched{t}"
-                    pair = sb.tile([P, 2, V], F32, name=f"fetched{d}{t}", tag=tag, align_bytes=64)
-                fetched[d, t] = pair[:, t % 2, :]
+                fetched[d, t] = third[:, t, :] if d == 1 else (first, second)[t // 2][:, t % 2, :]
                 nc.vector.tensor_copy(fetched[d, t], h[t][:].indirect(pos_t[d][:]))
         for d in range(D):
             for t in range(PACK):
                 acc = bank(2 * t + d)
                 product(acc[:], w3_q, slice(t * P, (t + 1) * P), a_q[d], slice(0, V))
-                if d == 0:
+                if d == 0 or t == 0:
                     filt = sb.tile([P, V], F32, name=f"filt{d}{t}")
                     nc.scalar.copy(filt[:], acc[:])
                     nc.gpsimd.tensor_tensor(prods[d][:, t, :], fetched[d, t], filt[:], MULT)

@@ -36,8 +36,8 @@ def tile_picked_dime_none_p_kernel(
             for r in range(4):
                 nc.sync.dma_start(plane[r:P:32, :].bitcast(I32), by_quadrant[r])
 
-        def load_rows(name, rows):
-            raw = sb.tile([P, PACK, rows.shape[1]], F32, name=name)
+        def load_rows(name, rows, pool=sb, **place):
+            raw = pool.tile([P, PACK, rows.shape[1]], F32, name=name, **place)
             nc.sync.dma_start(raw[:], rows.rearrange("(p j) c -> p j c", j=PACK))
             return raw
 
@@ -58,14 +58,15 @@ def tile_picked_dime_none_p_kernel(
                 stop=True,
             )
 
-        def deal_weight(name, raw, copy, t0, tiles, tag=None):
-            grouped = sb.tile([P, tiles * P * PACK], BF16, name=name + "_bf16", tag=tag or name + "_bf16", align_bytes=64)
+        def deal_weight(name, raw, copy, pair0, pairs, pool=sb, **place):
+            grouped = pool.tile([P, pairs * 2 * P * PACK], BF16, name=name + "_bf16", align_bytes=64, **place)
             copy(
-                out=grouped[:].rearrange("p (t m j) -> p m j t", t=tiles, j=PACK),
-                in_=raw[:].rearrange("p j (m t) -> p m j t", t=PACK)[:, :, :, t0 : t0 + tiles],
+                out=grouped[:].rearrange("p (u e m j) -> p u m j e", u=pairs, e=2, j=PACK),
+                in_=raw[:].rearrange("p j (m u e) -> p u m j e", u=2, e=2)[:, pair0 : pair0 + pairs],
             )
             return grouped
-        late = ctx.enter_context(tc.tile_pool(name="late", bufs=1))
+        early = ctx.enter_context(tc.tile_pool(name="early", bufs=1))
+        middle = ctx.enter_context(tc.tile_pool(name="middle", bufs=1))
 
         x_plane = sb.tile([P, T], U8, name="x_plane", align_bytes=64)
         nc.gpsimd.memset(x_plane[:].bitcast(I32), 0)
@@ -74,17 +75,21 @@ def tile_picked_dime_none_p_kernel(
         nc.scalar.activation(warm[:, 1:2], warm[:, 0:1], SILU)
         offs_t = sb.tile([P, S // 16], U16, name="offs_t")
         nc.sync.dma_start(offs_t[:], offs)
-        x_table = sb.tile([P, T], I32, name="x_table", align_bytes=64)
-        x_src = x_words[0].rearrange("p n t -> p (n t)").bitcast(I32)
-        nc.sync.dma_start(x_table[:, : T // 4], x_src[:, : T // 4])
+        w1_raw = sb.tile([P, PACK, H], F32, name="w1_raw")
+        w1_src = w1.rearrange("(p j) c -> p j c", j=PACK)
+        nc.sync.dma_start(w1_raw[:, 0:1, :], w1_src[:, 0:1, :])
         load_scale_rows(x_plane, x_scales)
-        nc.sync.dma_start(x_table[:, T // 4 :], x_src[:, T // 4 :])
-        w1_raw = load_rows("w1_raw", w1)
+        nc.sync.dma_start(w1_raw[:, 1:PACK, :], w1_src[:, 1:PACK, :])
+        x_table = sb.tile([P, T], I32, name="x_table", align_bytes=64)
+        nc.sync.dma_start(x_table[:], x_words[0].rearrange("p n t -> p (n t)").bitcast(I32))
         w3_raw = load_rows("w3_raw", w3)
         pos_t = [sb.tile([P, V // 16], U16, name=f"pos{d}_t") for d in range(D)]
         nc.sync.dma_start(pos_t[0][:], pos1)
         nc.sync.dma_start(pos_t[1][:], pos2)
-        a_raw = [load_rows(f"a_raw{d}", aT[:, d * V : (d + 1) * V]) for d in range(D)]
+        a_raw = [
+            load_rows("a_raw0", aT[:, :V], pool=middle, offset=0),
+            load_rows("a_raw1", aT[:, V:], pool=middle, offset=8192),
+        ]
         w2_codes = sb.tile([P, N], I32, name="w2_codes", align_bytes=64)
         nc.sync.dma_start(w2_codes[:], w2_words[0].rearrange("p n t -> p (n t)").bitcast(I32))
         w2_plane = sb.tile([P, N], U8, name="w2_plane", align_bytes=64)
@@ -93,6 +98,9 @@ def tile_picked_dime_none_p_kernel(
 
         picked_scales = sb.tile([P, S], U8, name="picked_scales", align_bytes=64)
         nc.vector.tensor_copy(picked_scales[:], x_plane[:].indirect(offs_t[:]))
+        w1_low = deal_weight("w1_low", w1_raw, nc.scalar.copy, 0, 1)
+        w1_high = deal_weight("w1_high", w1_raw, nc.vector.tensor_copy, 1, 1)
+        w1_q = [quantize("w1_low", w1_low[:], 2 * P), quantize("w1_high", w1_high[:], 2 * P)]
         words = []
         for half in range(S // BANK):
             picked = sb.tile([P, BANK], U32, name=f"picked_words{half}", align_bytes=64)
@@ -101,66 +109,78 @@ def tile_picked_dime_none_p_kernel(
             )
             words.append(picked)
 
-        w1_t0 = deal_weight("w1_t0", w1_raw, nc.scalar.copy, 0, 1, "w1_stage")
-        w1_t1 = deal_weight("w1_t1", w1_raw, nc.scalar.copy, 1, 1)
-        w1_q0 = quantize("w1_t0", w1_t0[:], P)
-        w1_high = deal_weight("w1_high", w1_raw, nc.vector.tensor_copy, 2, 2, "w1_stage")
-        w1_q1 = quantize("w1_t1", w1_t1[:], P)
-        w1_qh = quantize("w1_high", w1_high[:], 2 * P)
-        stat = [(w1_q0, 0), (w1_q1, 0), (w1_qh, 0), (w1_qh, P)]
+        h = [sb.tile([P, S], F32, name=f"h{t}") for t in range(2)]
+        h += [middle.tile([P, S], F32, name=f"h{t}", offset=(t - 2) * 8192) for t in range(2, PACK)]
 
-        h = [sb.tile([P, S], F32, name=f"h{t}") for t in range(PACK)]
-        for t in range(PACK):
-            (codes, scales), c0 = stat[t]
-            cols = slice(c0, c0 + P)
-            for half in range(S // BANK):
-                acc = bank(2 * t + half)
-                nc.tensor.matmul_mx(
-                    out=acc[:],
-                    lhsT=codes[:, cols].bitcast(FP8X4),
-                    lhsT_scale=scales[:, cols],
-                    rhs=words[half][:].bitcast(FP8X4),
-                    rhs_scale=picked_scales[:, half * BANK : (half + 1) * BANK],
-                    start=True,
-                    stop=True,
-                )
-                nc.scalar.activation(h[t][:, half * BANK : (half + 1) * BANK], acc[:], SILU)
-        w3_q = quantize("w3", deal_weight("w3", w3_raw, nc.vector.tensor_copy, 0, PACK)[:], H)
+        def hidden(t, half):
+            codes, scales = w1_q[t // 2]
+            cols = slice(t % 2 * P, (t % 2 + 1) * P)
+            acc = bank(2 * t + half)
+            nc.tensor.matmul_mx(
+                out=acc[:],
+                lhsT=codes[:, cols].bitcast(FP8X4),
+                lhsT_scale=scales[:, cols],
+                rhs=words[half][:].bitcast(FP8X4),
+                rhs_scale=picked_scales[:, half * BANK : (half + 1) * BANK],
+                start=True,
+                stop=True,
+            )
+            nc.scalar.activation(h[t][:, half * BANK : (half + 1) * BANK], acc[:], SILU)
 
-        a_q = []
-        for d in range(D):
-            if d == 0:
-                grouped = sb.tile([P, V, PACK], BF16, name="a_bf16_0", tag="a0_stage", align_bytes=64)
-                nc.gpsimd.tensor_scalar(grouped[:], a_raw[d][:].rearrange("p j v -> p v j"), 1.0, 0.0, MULT, ADD)
-            else:
-                grouped = late.tile([P, V, PACK], BF16, name="a_bf16_1", offset=6144, align_bytes=64)
-                nc.scalar.copy(
-                    out=grouped[:].rearrange("p (c i) j -> p c j i", i=4),
-                    in_=a_raw[d][:].rearrange("p j (c i) -> p c j i", i=4),
-                )
-            a_q.append(quantize(f"a{d}", grouped[:].rearrange("p v j -> p (v j)"), V))
+        def interleave(copy, stage, d, cols):
+            copy(
+                out=stage[:, cols, :].rearrange("p (c i) j -> p c j i", i=4),
+                in_=a_raw[d][:, :, cols].rearrange("p j (c i) -> p c j i", i=4),
+            )
+
+        def filters(d, t, a_q):
+            acc = bank(t if d == 0 else PACK + t % 2)
+            product(acc[:], w3_q, slice(t * P, (t + 1) * P), a_q, slice(0, V))
+            return acc
+
+        for half in range(2):
+            for t in range(2):
+                hidden(t, half)
+        w3_q = quantize("w3", deal_weight("w3", w3_raw, nc.vector.tensor_copy, 0, 2, pool=early, offset=0)[:], H)
+        a0_stage = sb.tile([P, V, PACK], BF16, name="a0_stage", tag="a_stage", align_bytes=64)
+        interleave(nc.scalar.copy, a0_stage, 0, slice(0, V))
+        a0_q = quantize("a0", a0_stage[:].rearrange("p v j -> p (v j)"), V)
+        a1_stage = sb.tile([P, V, PACK], BF16, name="a1_stage", tag="a_stage", align_bytes=64)
+        interleave(nc.vector.tensor_copy, a1_stage, 1, slice(0, V // 2))
+        for half in range(2):
+            hidden(2, half)
+
+        last = PACK - 1
+        fetched = early.tile([P, last, V], F32, name="fetched", offset=0, align_bytes=64)
+        for t in range(last):
+            nc.vector.tensor_copy(fetched[:, t, :], h[t][:].indirect(pos_t[1][:]))
+
         prods = [
-            late.tile([P, PACK, V], F32, name="prod0", offset=8192, align_bytes=64),
+            sb.tile([P, PACK, V], F32, name="prod0"),
             sb.tile([P, PACK, V], F32, name="prod1"),
         ]
-        first = sb.tile([P, 2, V], F32, name="fetched_first", align_bytes=64)
-        second = sb.tile([P, 2, V], F32, name="fetched_second", tag="a0_stage", align_bytes=64)
-        third = late.tile([P, PACK, V], F32, name="fetched_third", offset=0, align_bytes=64)
-        fetched = {}
-        for d in range(D):
-            for t in range(PACK):
-                fetched[d, t] = third[:, t, :] if d == 1 else (first, second)[t // 2][:, t % 2, :]
-                nc.vector.tensor_copy(fetched[d, t], h[t][:].indirect(pos_t[d][:]))
-        for d in range(D):
-            for t in range(PACK):
-                acc = bank(2 * t + d)
-                product(acc[:], w3_q, slice(t * P, (t + 1) * P), a_q[d], slice(0, V))
-                if d == 0 or t == 0:
-                    filt = sb.tile([P, V], F32, name=f"filt{d}{t}")
-                    nc.scalar.copy(filt[:], acc[:])
-                    nc.gpsimd.tensor_tensor(prods[d][:, t, :], fetched[d, t], filt[:], MULT)
-                else:
-                    nc.vector.tensor_tensor(prods[d][:, t, :], fetched[d, t], acc[:], MULT)
+
+        staged = sb.tile([P, PACK, V], F32, name="staged")
+
+        def fused_term(d, t, a_q):
+            filt = staged[:, t, :] if d == 0 else prods[1][:, 2, :]
+            nc.scalar.copy(filt, filters(d, t, a_q)[:])
+            nc.vector.tensor_tensor(prods[d][:, t, :], h[t][:].indirect(pos_t[d][:]), filt, MULT)
+
+        fused_term(0, 0, a0_q)
+        fused_term(0, 1, a0_q)
+        interleave(nc.scalar.copy, a1_stage, 1, slice(V // 2, V))
+        a1_q = quantize("a1", a1_stage[:].rearrange("p v j -> p (v j)"), V)
+        for half in range(2):
+            hidden(last, half)
+        fused_term(0, 2, a0_q)
+        fused_term(0, last, a0_q)
+        fused_term(1, last, a1_q)
+        filt = sb.tile([P, V], F32, name="filt_last")
+        nc.scalar.copy(filt[:], filters(1, 2, a1_q)[:])
+        nc.gpsimd.tensor_tensor(prods[1][:, 2, :], fetched[:, 2, :], filt[:], MULT)
+        for t in (1, 0):
+            nc.vector.tensor_tensor(prods[1][:, t, :], fetched[:, t, :], filters(1, t, a1_q)[:], MULT)
 
         lo = 0
         for part, width in enumerate((256, 128, 128)):

@@ -41,8 +41,8 @@ def tile_picked_dime_none_p_kernel(
             nc.sync.dma_start(raw[:], rows.rearrange("(p j) c -> p j c", j=PACK))
             return raw
 
-        def quantize(name, grouped, width):
-            codes = sb.tile([P, width], U32, name=name + "_codes", align_bytes=64)
+        def quantize(name, grouped, width, pool=sb, **place):
+            codes = pool.tile([P, width], U32, name=name + "_codes", align_bytes=64, **place)
             scales = sb.tile([P, width], U8, name=name + "_scales", align_bytes=64)
             nc.vector.quantize_mx(out=codes[:].bitcast(FP8X4), scales=scales[:], in_=grouped)
             return codes, scales
@@ -134,19 +134,22 @@ def tile_picked_dime_none_p_kernel(
             )
 
         def filters(d, t, a_q):
-            acc = bank(t if d == 0 else PACK + t % 2)
-            product(acc[:], w3_q, slice(t * P, (t + 1) * P), a_q, slice(0, V))
+            acc = bank(t if d == 0 else (6, 4, 5, 5)[t])
+            product(acc[:], w3_q[t // 2], slice(t % 2 * P, (t % 2 + 1) * P), a_q, slice(0, V))
             return acc
 
         for half in range(2):
             for t in range(2):
                 hidden(t, half)
-        w3_q = quantize("w3", deal_weight("w3", w3_raw, nc.vector.tensor_copy, 0, 2, pool=early, offset=0)[:], H)
+        w3_stage = [
+            deal_weight(f"w3_{u}", w3_raw, nc.vector.tensor_copy, u, 1, pool=early, offset=2048 * u) for u in range(2)
+        ]
+        w3_q = [quantize(f"w3_{u}", w3_stage[u][:], 2 * P) for u in range(2)]
         a0_stage = sb.tile([P, V, PACK], BF16, name="a0_stage", tag="a_stage", align_bytes=64)
         interleave(nc.scalar.copy, a0_stage, 0, slice(0, V))
         a0_q = quantize("a0", a0_stage[:].rearrange("p v j -> p (v j)"), V)
         a1_stage = sb.tile([P, V, PACK], BF16, name="a1_stage", tag="a_stage", align_bytes=64)
-        interleave(nc.vector.tensor_copy, a1_stage, 1, slice(0, V // 2))
+        interleave(nc.vector.tensor_copy, a1_stage, 1, slice(0, 352))
         for half in range(2):
             hidden(2, half)
 
@@ -163,39 +166,53 @@ def tile_picked_dime_none_p_kernel(
         staged = sb.tile([P, PACK, V], F32, name="staged")
 
         def fused_term(d, t, a_q):
-            filt = staged[:, t, :] if d == 0 else prods[1][:, 2, :]
+            filt = staged[:, t, :] if d == 0 else prods[1][:].rearrange("p t v -> p (t v)")[:, V // 2 : V // 2 + V]
             nc.scalar.copy(filt, filters(d, t, a_q)[:])
             nc.vector.tensor_tensor(prods[d][:, t, :], h[t][:].indirect(pos_t[d][:]), filt, MULT)
 
         fused_term(0, 0, a0_q)
         fused_term(0, 1, a0_q)
-        interleave(nc.scalar.copy, a1_stage, 1, slice(V // 2, V))
+        interleave(nc.scalar.copy, a1_stage, 1, slice(352, V))
         a1_q = quantize("a1", a1_stage[:].rearrange("p v j -> p (v j)"), V)
         for half in range(2):
             hidden(last, half)
         fused_term(0, 2, a0_q)
         fused_term(0, last, a0_q)
         fused_term(1, last, a1_q)
-        filt = sb.tile([P, V], F32, name="filt_last")
-        nc.scalar.copy(filt[:], filters(1, 2, a1_q)[:])
-        nc.gpsimd.tensor_tensor(prods[1][:, 2, :], fetched[:, 2, :], filt[:], MULT)
-        for t in (1, 0):
+        shared = filters(1, 1, a1_q)
+        on_vector, on_gpsimd = slice(0, 192), slice(192, V)
+        filt = sb.tile([P, V - 192], F32, name="filt_last")
+        nc.scalar.copy(filt[:], shared[:, on_gpsimd])
+        nc.gpsimd.tensor_tensor(prods[1][:, 1, on_gpsimd], fetched[:, 1, on_gpsimd], filt[:], MULT)
+        for t in (2, 0):
             nc.vector.tensor_tensor(prods[1][:, t, :], fetched[:, t, :], filters(1, t, a1_q)[:], MULT)
+        nc.vector.tensor_tensor(prods[1][:, 1, on_vector], fetched[:, 1, on_vector], shared[:, on_vector], MULT)
 
-        lo = 0
-        for part, width in enumerate((256, 128, 128)):
-            cols = slice(lo, lo + width)
-            lo = lo + width
-            z = sb.tile([P, width, PACK], BF16, name=f"z{part}", align_bytes=64)
+        parts = [slice(256, 512), slice(0, 128), slice(128, 256)]
+
+        def add_terms(part):
+            cols = parts[part]
+            z = sb.tile([P, cols.stop - cols.start, PACK], BF16, name=f"z{part}", align_bytes=64)
             nc.vector.tensor_tensor(
                 z[:].rearrange("p (c i) t -> p c t i", i=4),
                 prods[0][:, :, cols].rearrange("p t (c i) -> p c t i", i=4),
                 prods[1][:, :, cols].rearrange("p t (c i) -> p c t i", i=4),
                 ADD,
             )
+            return z
+
+        def project(part, z):
+            cols = parts[part]
+            width = cols.stop - cols.start
             z_q = quantize(f"z{part}", z[:].rearrange("p v t -> p (v t)"), width)
             acc = bank(part)
             product(acc[:, 0:width], (w2_codes, w2_plane), slice(0, N), z_q, slice(0, width))
             result = sb.tile([P, width], F32, name=f"result{part}")
             nc.scalar.copy(result[:], acc[:, 0:width])
             nc.scalar.dma_start(out[:, cols], result[:])
+
+        z = [add_terms(0), add_terms(1)]
+        project(0, z[0])
+        z.append(add_terms(2))
+        project(1, z[1])
+        project(2, z[2])

@@ -142,21 +142,26 @@ def tile_picked_dime_none_p_kernel(
             for t in range(2):
                 hidden(t, half)
         w3_stage = [
-            deal_weight(f"w3_{u}", w3_raw, nc.vector.tensor_copy, u, 1, pool=early, offset=2048 * u) for u in range(2)
+            deal_weight(f"w3_{u}", w3_raw, nc.vector.tensor_copy, u, 1, pool=early, offset=3072 * u) for u in range(2)
         ]
         w3_q = [quantize(f"w3_{u}", w3_stage[u][:], 2 * P) for u in range(2)]
-        a0_stage = sb.tile([P, V, PACK], BF16, name="a0_stage", tag="a_stage", align_bytes=64)
-        interleave(nc.scalar.copy, a0_stage, 0, slice(0, V))
+        a0_stage = early.tile([P, V, PACK], BF16, name="a0_stage", offset=4096, align_bytes=64)
+        nc.gpsimd.tensor_scalar(
+            a0_stage[:, :192, :], a_raw[0][:, :, :192].rearrange("p j v -> p v j"), 1.0, 0.0, MULT, ADD
+        )
+        interleave(nc.scalar.copy, a0_stage, 0, slice(192, V))
         a0_q = quantize("a0", a0_stage[:].rearrange("p v j -> p (v j)"), V)
-        a1_stage = sb.tile([P, V, PACK], BF16, name="a1_stage", tag="a_stage", align_bytes=64)
-        interleave(nc.vector.tensor_copy, a1_stage, 1, slice(0, 352))
         for half in range(2):
             hidden(2, half)
+        a1_stage = sb.tile([P, V, PACK], BF16, name="a1_stage", align_bytes=64)
+        interleave(nc.scalar.copy, a1_stage, 1, slice(0, 192))
 
         last = PACK - 1
-        fetched = early.tile([P, last, V], F32, name="fetched", offset=0, align_bytes=64)
+        first = early.tile([P, 2, V], F32, name="fetched_first", offset=0, align_bytes=64)
+        third = early.tile([P, V], F32, name="fetched_third", offset=4096, align_bytes=64)
+        fetched = [first[:, 0, :], first[:, 1, :], third[:]]
         for t in range(last):
-            nc.vector.tensor_copy(fetched[:, t, :], h[t][:].indirect(pos_t[1][:]))
+            nc.vector.tensor_copy(fetched[t], h[t][:].indirect(pos_t[1][:]))
 
         prods = [
             sb.tile([P, PACK, V], F32, name="prod0"),
@@ -172,21 +177,21 @@ def tile_picked_dime_none_p_kernel(
 
         fused_term(0, 0, a0_q)
         fused_term(0, 1, a0_q)
-        interleave(nc.scalar.copy, a1_stage, 1, slice(352, V))
+        interleave(nc.scalar.copy, a1_stage, 1, slice(192, V))
         a1_q = quantize("a1", a1_stage[:].rearrange("p v j -> p (v j)"), V)
+        fused_term(0, 2, a0_q)
         for half in range(2):
             hidden(last, half)
-        fused_term(0, 2, a0_q)
         fused_term(0, last, a0_q)
         fused_term(1, last, a1_q)
         shared = filters(1, 1, a1_q)
         on_vector, on_gpsimd = slice(0, 192), slice(192, V)
         filt = sb.tile([P, V - 192], F32, name="filt_last")
         nc.scalar.copy(filt[:], shared[:, on_gpsimd])
-        nc.gpsimd.tensor_tensor(prods[1][:, 1, on_gpsimd], fetched[:, 1, on_gpsimd], filt[:], MULT)
+        nc.gpsimd.tensor_tensor(prods[1][:, 1, on_gpsimd], fetched[1][:, on_gpsimd], filt[:], MULT)
         for t in (2, 0):
-            nc.vector.tensor_tensor(prods[1][:, t, :], fetched[:, t, :], filters(1, t, a1_q)[:], MULT)
-        nc.vector.tensor_tensor(prods[1][:, 1, on_vector], fetched[:, 1, on_vector], shared[:, on_vector], MULT)
+            nc.vector.tensor_tensor(prods[1][:, t, :], fetched[t], filters(1, t, a1_q)[:], MULT)
+        nc.vector.tensor_tensor(prods[1][:, 1, on_vector], fetched[1][:, on_vector], shared[:, on_vector], MULT)
 
         parts = [slice(256, 512), slice(0, 128), slice(128, 256)]
 

@@ -1,6 +1,7 @@
 from contextlib import ExitStack
 
 import concourse.mybir as mybir
+from concourse.masks import make_identity
 
 F32 = mybir.dt.float32
 BF16 = mybir.dt.bfloat16
@@ -66,6 +67,7 @@ def tile_picked_dime_none_p_kernel(
             )
             return grouped
         early = ctx.enter_context(tc.tile_pool(name="early", bufs=1))
+        late_pool = ctx.enter_context(tc.tile_pool(name="late", bufs=1))
         middle = ctx.enter_context(tc.tile_pool(name="middle", bufs=1))
 
         x_plane = sb.tile([P, T], U8, name="x_plane", align_bytes=64)
@@ -95,6 +97,9 @@ def tile_picked_dime_none_p_kernel(
         w2_plane = sb.tile([P, N], U8, name="w2_plane", align_bytes=64)
         nc.gpsimd.memset(w2_plane[:], 0)
         load_scale_rows(w2_plane, w2_scales)
+
+        ident = sb.tile([P, P], F32, name="ident")
+        make_identity(nc, ident[:])
 
         picked_scales = sb.tile([P, S], U8, name="picked_scales", align_bytes=64)
         nc.vector.tensor_copy(picked_scales[:], x_plane[:].indirect(offs_t[:]))
@@ -134,7 +139,7 @@ def tile_picked_dime_none_p_kernel(
             )
 
         def filters(d, t, a_q):
-            acc = bank(t if d == 0 else (6, 4, 5, 5)[t])
+            acc = bank((t + 1) % PACK)
             product(acc[:], w3_q[t // 2], slice(t % 2 * P, (t % 2 + 1) * P), a_q, slice(0, V))
             return acc
 
@@ -163,61 +168,132 @@ def tile_picked_dime_none_p_kernel(
         for t in range(last):
             nc.vector.tensor_copy(fetched[t], h[t][:].indirect(pos_t[1][:]))
 
-        prods = [
-            sb.tile([P, PACK, V], F32, name="prod0"),
-            sb.tile([P, PACK, V], F32, name="prod1"),
-        ]
+        first_terms = sb.tile([P, PACK, V], F32, name="first_terms")
+        second_a = sb.tile([P, PACK, V // 2], F32, name="second_a")
+        second_b = late_pool.tile([P, PACK, V // 2], F32, name="second_b", offset=0)
+
+        def term(d, tiles, cols):
+            if d == 0:
+                return first_terms[:, tiles, cols]
+            if cols.stop <= V // 2:
+                return second_a[:, tiles, cols]
+            return second_b[:, tiles, cols.start - V // 2 : cols.stop - V // 2]
 
         staged = sb.tile([P, PACK, V], F32, name="staged")
 
-        def fused_term(d, t, a_q):
-            filt = staged[:, t, :] if d == 0 else prods[1][:].rearrange("p t v -> p (t v)")[:, V // 2 : V // 2 + V]
-            nc.scalar.copy(filt, filters(d, t, a_q)[:])
-            nc.vector.tensor_tensor(prods[d][:, t, :], h[t][:].indirect(pos_t[d][:]), filt, MULT)
+        half_a, half_b = slice(0, V // 2), slice(V // 2, V)
 
-        fused_term(0, 0, a0_q)
-        fused_term(0, 1, a0_q)
+        def offsets(d, cols):
+            return pos_t[d][:, cols.start // 16 : cols.stop // 16]
+
+        def fused_term(d, t, filt, cols):
+            nc.vector.tensor_tensor(term(d, t, cols), h[t][:].indirect(offsets(d, cols)), filt, MULT)
+
+        def psum_term(t, cols):
+            nc.vector.tensor_tensor(term(1, t, cols), fetched[t][:, cols], late[t, cols.start // (V // 2)], MULT)
+
+        def stage_filter(d, t, a_q):
+            nc.scalar.copy(staged[:, t, :], filters(d, t, a_q)[:])
+            return staged[:, t, :]
+
+        whole = slice(0, V)
+        for k, cols in enumerate((half_a, half_b)):
+            acc = bank(k)
+            product(acc[:, : V // 2], w3_q[0], slice(0, P), a0_q, cols)
+            nc.scalar.copy(staged[:, 0, cols], acc[:, : V // 2])
+            fused_term(0, 0, staged[:, 0, cols], cols)
+        fused_term(0, 1, stage_filter(0, 1, a0_q), whole)
         interleave(nc.scalar.copy, a1_stage, 1, slice(192, V))
         a1_q = quantize("a1", a1_stage[:].rearrange("p v j -> p (v j)"), V)
-        fused_term(0, 2, a0_q)
+        filt02 = stage_filter(0, 2, a0_q)
+        fused_term(0, 2, filt02[:, half_a], half_a)
         for half in range(2):
             hidden(last, half)
-        fused_term(0, last, a0_q)
-        fused_term(1, last, a1_q)
-        shared = filters(1, 1, a1_q)
-        on_vector, on_gpsimd = slice(0, 192), slice(192, V)
-        filt = sb.tile([P, V - 192], F32, name="filt_last")
-        nc.scalar.copy(filt[:], shared[:, on_gpsimd])
-        nc.gpsimd.tensor_tensor(prods[1][:, 1, on_gpsimd], fetched[1][:, on_gpsimd], filt[:], MULT)
-        for t in (2, 0):
-            nc.vector.tensor_tensor(prods[1][:, t, :], fetched[t], filters(1, t, a1_q)[:], MULT)
-        nc.vector.tensor_tensor(prods[1][:, 1, on_vector], fetched[1][:, on_vector], shared[:, on_vector], MULT)
+        bank03 = filters(0, last, a0_q)
+        late = {}
+        for k, cols in enumerate((half_a, half_b)):
+            for u in range(2):
+                acc = bank(PACK + 2 * k + u)
+                for e in range(2):
+                    late[2 * u + e, k] = acc[:, e * (V // 2) : (e + 1) * (V // 2)]
+                    product(late[2 * u + e, k], w3_q[u], slice(e * P, (e + 1) * P), a1_q, cols)
+        filt03_a, filt13_a = staged[:, last, half_a], first_terms[:, 2, half_b]
+        filt03_b = late_pool.tile([P, V // 2], F32, name="filt03_b", offset=0)
+        filt13_b = staged[:, last, half_b]
+        nc.scalar.copy(filt03_a, bank03[:, half_a])
+        nc.scalar.copy(filt13_a, late[last, 0])
+        nc.scalar.copy(filt03_b[:], bank03[:, half_b])
+        nc.scalar.copy(filt13_b, late[last, 1])
 
-        parts = [slice(256, 512), slice(0, 128), slice(128, 256)]
+        chunks = [slice(0, P), slice(P, 2 * P)]
+        summed = [bank(1 + c) for c in range(2)]
 
-        def add_terms(part):
-            cols = parts[part]
-            z = sb.tile([P, cols.stop - cols.start, PACK], BF16, name=f"z{part}", align_bytes=64)
+        def add_on_tensor(t):
+            for c in range(2):
+                for d in range(D):
+                    nc.tensor.matmul(
+                        summed[c][:, t * P : (t + 1) * P],
+                        term(d, t, chunks[c]),
+                        ident[:],
+                        start=(d == 0),
+                        stop=(d == D - 1),
+                        is_transpose=True,
+                    )
+
+        psum_term(0, half_a)
+        psum_term(1, half_a)
+        fused_term(0, last, filt03_a, half_a)
+        psum_term(2, half_a)
+        fused_term(1, last, filt13_a, half_a)
+        for t in range(PACK):
+            add_on_tensor(t)
+        fused_term(0, 2, filt02[:, half_b], half_b)
+        fused_term(0, last, filt03_b[:], half_b)
+        fused_term(1, last, filt13_b, half_b)
+        for t in range(last):
+            psum_term(t, half_b)
+
+        back = bank(3)
+        for c in range(2):
+            turned = sb.tile([P, H], BF16, name=f"turned{c}")
+            nc.scalar.copy(
+                out=turned[:].rearrange("p (u q e) -> p u q e", u=2, e=2),
+                in_=summed[c][:].rearrange("p (u e q) -> p u q e", u=2, e=2),
+            )
+            for u in range(2):
+                nc.tensor.transpose(
+                    back[:, (2 * c + u) * P : (2 * c + u + 1) * P],
+                    turned[:].bitcast(F32)[:, u * P : (u + 1) * P],
+                    ident[:],
+                )
+        z_a = sb.tile([P, V // 2 * PACK], BF16, name="z_a", align_bytes=64)
+        nc.scalar.copy(
+            out=z_a[:].bitcast(F32).rearrange("p (c v u) -> p c v u", c=2, u=2),
+            in_=back[:].rearrange("p (c u v) -> p c v u", c=2, u=2),
+        )
+
+        def add_terms(name, cols):
+            z = sb.tile([P, cols.stop - cols.start, PACK], BF16, name=name, align_bytes=64)
             nc.vector.tensor_tensor(
                 z[:].rearrange("p (c i) t -> p c t i", i=4),
-                prods[0][:, :, cols].rearrange("p t (c i) -> p c t i", i=4),
-                prods[1][:, :, cols].rearrange("p t (c i) -> p c t i", i=4),
+                term(0, slice(0, PACK), cols).rearrange("p t (c i) -> p c t i", i=4),
+                term(1, slice(0, PACK), cols).rearrange("p t (c i) -> p c t i", i=4),
                 ADD,
             )
-            return z
+            return z[:].rearrange("p v t -> p (v t)")
 
-        def project(part, z):
-            cols = parts[part]
+        def project(name, z, cols, b):
             width = cols.stop - cols.start
-            z_q = quantize(f"z{part}", z[:].rearrange("p v t -> p (v t)"), width)
-            acc = bank(part)
+            z_q = quantize(name, z, width)
+            acc = bank(b)
             product(acc[:, 0:width], (w2_codes, w2_plane), slice(0, N), z_q, slice(0, width))
-            result = sb.tile([P, width], F32, name=f"result{part}")
+            result = sb.tile([P, width], F32, name=name + "_result")
             nc.scalar.copy(result[:], acc[:, 0:width])
             nc.scalar.dma_start(out[:, cols], result[:])
 
-        z = [add_terms(0), add_terms(1)]
-        project(0, z[0])
-        z.append(add_terms(2))
-        project(1, z[1])
-        project(2, z[2])
+        parts = [slice(256, 384), slice(384, 512)]
+        z_b0 = add_terms("z_b0", parts[0])
+        project("z_a", z_a[:], half_a, 0)
+        z_b1 = add_terms("z_b1", parts[1])
+        project("z_b0", z_b0, parts[0], 1)
+        project("z_b1", z_b1, parts[1], 2)

@@ -32,10 +32,10 @@ def tile_picked_dime_none_p_kernel(
         def bank(b):
             return psum.tile([P, BANK], F32, name=f"bank{b}")
 
-        def load_scale_rows(plane, rows):
+        def load_scale_rows(plane, rows, queue=nc.sync):
             by_quadrant = rows[0].bitcast(I32).rearrange("(q r) c -> r q c", r=4)
             for r in range(4):
-                nc.sync.dma_start(plane[r:P:32, :].bitcast(I32), by_quadrant[r])
+                queue.dma_start(plane[r:P:32, :].bitcast(I32), by_quadrant[r])
 
         def load_rows(name, rows, pool=sb, **place):
             raw = pool.tile([P, PACK, rows.shape[1]], F32, name=name, **place)
@@ -86,11 +86,12 @@ def tile_picked_dime_none_p_kernel(
         nc.sync.dma_start(x_table[:], x_words[0].rearrange("p n t -> p (n t)").bitcast(I32))
         w3_raw = load_rows("w3_raw", w3)
         pos_t = [sb.tile([P, V // 16], U16, name=f"pos{d}_t") for d in range(D)]
-        nc.sync.dma_start(pos_t[0][:], pos1)
         nc.sync.dma_start(pos_t[1][:], pos2)
-        a_raw = [
-            load_rows("a_raw0", aT[:, :V], pool=middle, offset=0),
-            load_rows("a_raw1", aT[:, V:], pool=middle, offset=8192),
+        a0_raw = load_rows("a0_raw", aT[:, :V], pool=middle, offset=0)
+        nc.sync.dma_start(pos_t[0][:], pos1)
+        a1_raw = [
+            load_rows("a1_raw0", aT[:, V : V + V // 2]),
+            load_rows("a1_raw1", aT[:, V + V // 2 :], pool=middle, offset=8192),
         ]
         w2_codes = sb.tile([P, N], I32, name="w2_codes", align_bytes=64)
         nc.sync.dma_start(w2_codes[:], w2_words[0].rearrange("p n t -> p (n t)").bitcast(I32))
@@ -132,10 +133,10 @@ def tile_picked_dime_none_p_kernel(
             )
             nc.scalar.activation(h[t][:, half * BANK : (half + 1) * BANK], acc[:], SILU)
 
-        def interleave(copy, stage, d, cols):
-            copy(
-                out=stage[:, cols, :].rearrange("p (c i) j -> p c j i", i=4),
-                in_=a_raw[d][:, :, cols].rearrange("p j (c i) -> p c j i", i=4),
+        def interleave(stage, raw):
+            nc.scalar.copy(
+                out=stage.rearrange("p (c i) j -> p c j i", i=4),
+                in_=raw.rearrange("p j (c i) -> p c j i", i=4),
             )
 
         def filters(d, t, a_q):
@@ -152,14 +153,14 @@ def tile_picked_dime_none_p_kernel(
         w3_q = [quantize(f"w3_{u}", w3_stage[u][:], 2 * P) for u in range(2)]
         a0_stage = early.tile([P, V, PACK], BF16, name="a0_stage", offset=4096, align_bytes=64)
         nc.gpsimd.tensor_scalar(
-            a0_stage[:, :192, :], a_raw[0][:, :, :192].rearrange("p j v -> p v j"), 1.0, 0.0, MULT, ADD
+            a0_stage[:, :240, :], a0_raw[:, :, :240].rearrange("p j v -> p v j"), 1.0, 0.0, MULT, ADD
         )
-        interleave(nc.scalar.copy, a0_stage, 0, slice(192, V))
+        interleave(a0_stage[:, 240:, :], a0_raw[:, :, 240:])
         a0_q = quantize("a0", a0_stage[:].rearrange("p v j -> p (v j)"), V)
         for half in range(2):
             hidden(2, half)
         a1_stage = sb.tile([P, V, PACK], BF16, name="a1_stage", align_bytes=64)
-        interleave(nc.scalar.copy, a1_stage, 1, slice(0, 192))
+        interleave(a1_stage[:, : V // 2, :], a1_raw[0][:])
 
         last = PACK - 1
         first = early.tile([P, 2, V], F32, name="fetched_first", offset=0, align_bytes=64)
@@ -203,7 +204,7 @@ def tile_picked_dime_none_p_kernel(
             nc.scalar.copy(staged[:, 0, cols], acc[:, : V // 2])
             fused_term(0, 0, staged[:, 0, cols], cols)
         fused_term(0, 1, stage_filter(0, 1, a0_q), whole)
-        interleave(nc.scalar.copy, a1_stage, 1, slice(192, V))
+        interleave(a1_stage[:, V // 2 :, :], a1_raw[1][:])
         a1_q = quantize("a1", a1_stage[:].rearrange("p v j -> p (v j)"), V)
         filt02 = stage_filter(0, 2, a0_q)
         fused_term(0, 2, filt02[:, half_a], half_a)
@@ -226,54 +227,54 @@ def tile_picked_dime_none_p_kernel(
         nc.scalar.copy(filt13_b, late[last, 1])
 
         chunks = [slice(0, P), slice(P, 2 * P)]
-        summed = [bank(1 + c) for c in range(2)]
+        low_pair = bank(1)
+        back = bank(3)
 
-        def add_on_tensor(t):
-            for c in range(2):
-                for d in range(D):
-                    nc.tensor.matmul(
-                        summed[c][:, t * P : (t + 1) * P],
-                        term(d, t, chunks[c]),
-                        ident[:],
-                        start=(d == 0),
-                        stop=(d == D - 1),
-                        is_transpose=True,
-                    )
+        def add_on_tensor(acc, d, t, c):
+            nc.tensor.matmul(acc, term(d, t, chunks[c]), ident[:], start=(d == 0), stop=(d == D - 1), is_transpose=True)
+
+        def turn_back(name, sums, places):
+            turned = sb.tile([P, len(places), 2 * P], BF16, name=name)
+            nc.scalar.copy(
+                out=turned[:].rearrange("p c (q e) -> p c q e", e=2),
+                in_=sums.rearrange("p (c e q) -> p c q e", c=len(places), e=2),
+            )
+            for k, place in enumerate(places):
+                nc.tensor.transpose(back[:, place * P : (place + 1) * P], turned[:, k, :].bitcast(F32), ident[:])
 
         psum_term(0, half_a)
         psum_term(1, half_a)
+        for c in range(2):
+            for t in range(2):
+                for d in range(D):
+                    add_on_tensor(low_pair[:, (2 * c + t) * P : (2 * c + t + 1) * P], d, t, c)
         fused_term(0, last, filt03_a, half_a)
         psum_term(2, half_a)
+        high_pair = [bank(2), bank(PACK)]
+        for c in range(2):
+            for d in range(D):
+                add_on_tensor(high_pair[c][:, :P], d, 2, c)
+            add_on_tensor(high_pair[c][:, P : 2 * P], 0, last, c)
         fused_term(1, last, filt13_a, half_a)
-        for t in range(PACK):
-            add_on_tensor(t)
+        for c in range(2):
+            add_on_tensor(high_pair[c][:, P : 2 * P], 1, last, c)
+        turn_back("turned_low", low_pair[:], [0, 2])
+        for c in range(2):
+            turn_back(f"turned_high{c}", high_pair[c][:, : 2 * P], [2 * c + 1])
         fused_term(0, 2, filt02[:, half_b], half_b)
         fused_term(0, last, filt03_b[:], half_b)
         fused_term(1, last, filt13_b, half_b)
         for t in range(last):
             psum_term(t, half_b)
 
-        back = bank(3)
-        for c in range(2):
-            turned = sb.tile([P, H], BF16, name=f"turned{c}")
-            nc.scalar.copy(
-                out=turned[:].rearrange("p (u q e) -> p u q e", u=2, e=2),
-                in_=summed[c][:].rearrange("p (u e q) -> p u q e", u=2, e=2),
-            )
-            for u in range(2):
-                nc.tensor.transpose(
-                    back[:, (2 * c + u) * P : (2 * c + u + 1) * P],
-                    turned[:].bitcast(F32)[:, u * P : (u + 1) * P],
-                    ident[:],
-                )
-        z_a = sb.tile([P, V // 2 * PACK], BF16, name="z_a", align_bytes=64)
+        z_a = late_pool.tile([P, V // 2 * PACK], BF16, name="z_a", offset=4096, align_bytes=64)
         nc.scalar.copy(
             out=z_a[:].bitcast(F32).rearrange("p (c v u) -> p c v u", c=2, u=2),
             in_=back[:].rearrange("p (c u v) -> p c v u", c=2, u=2),
         )
 
         def add_terms(name, cols):
-            z = sb.tile([P, cols.stop - cols.start, PACK], BF16, name=name, align_bytes=64)
+            z = late_pool.tile([P, P, PACK], BF16, name=name, offset=4096 + 8 * (cols.start - V // 2), align_bytes=64)
             nc.vector.tensor_tensor(
                 z[:].rearrange("p (c i) t -> p c t i", i=4),
                 term(0, slice(0, PACK), cols).rearrange("p t (c i) -> p c t i", i=4),
@@ -292,8 +293,8 @@ def tile_picked_dime_none_p_kernel(
             nc.scalar.dma_start(out[:, cols], result[:])
 
         parts = [slice(256, 384), slice(384, 512)]
-        z_b0 = add_terms("z_b0", parts[0])
         project("z_a", z_a[:], half_a, 0)
+        z_b0 = add_terms("z_b0", parts[0])
         z_b1 = add_terms("z_b1", parts[1])
         project("z_b0", z_b0, parts[0], 1)
         project("z_b1", z_b1, parts[1], 2)

@@ -90,8 +90,8 @@ def tile_picked_dime_none_p_kernel(
         a0_raw = load_rows("a0_raw", aT[:, :V], pool=middle, offset=0)
         nc.sync.dma_start(pos_t[0][:], pos1)
         a1_raw = [
-            load_rows("a1_raw0", aT[:, V : V + V // 2]),
-            load_rows("a1_raw1", aT[:, V + V // 2 :], pool=middle, offset=8192),
+            load_rows("a1_raw0", aT[:, V : V + 320]),
+            load_rows("a1_raw1", aT[:, V + 320 :], pool=middle, offset=8192),
         ]
         w2_codes = sb.tile([P, N], I32, name="w2_codes", align_bytes=64)
         nc.sync.dma_start(w2_codes[:], w2_words[0].rearrange("p n t -> p (n t)").bitcast(I32))
@@ -116,7 +116,7 @@ def tile_picked_dime_none_p_kernel(
             words.append(picked)
 
         h = [sb.tile([P, S], F32, name=f"h{t}") for t in range(2)]
-        h += [middle.tile([P, S], F32, name=f"h{t}", offset=(t - 2) * 8192) for t in range(2, PACK)]
+        h += [middle.tile([P, S], F32, name=f"h{t}", offset=(t - 2) * 5120) for t in range(2, PACK)]
 
         def hidden(t, half):
             codes, scales = w1_q[t // 2]
@@ -148,37 +148,39 @@ def tile_picked_dime_none_p_kernel(
             for t in range(2):
                 hidden(t, half)
         w3_stage = [
-            deal_weight(f"w3_{u}", w3_raw, nc.vector.tensor_copy, u, 1, pool=early, offset=3072 * u) for u in range(2)
+            deal_weight(f"w3_{u}", w3_raw, nc.vector.tensor_copy, u, 1, pool=early, offset=5120 * u) for u in range(2)
         ]
         w3_q = [quantize(f"w3_{u}", w3_stage[u][:], 2 * P) for u in range(2)]
-        a0_stage = early.tile([P, V, PACK], BF16, name="a0_stage", offset=4096, align_bytes=64)
+        a0_stage = early.tile([P, V, PACK], BF16, name="a0_stage", offset=6144, align_bytes=64)
         nc.gpsimd.tensor_scalar(
-            a0_stage[:, :240, :], a0_raw[:, :, :240].rearrange("p j v -> p v j"), 1.0, 0.0, MULT, ADD
+            a0_stage[:, :192, :], a0_raw[:, :, :192].rearrange("p j v -> p v j"), 1.0, 0.0, MULT, ADD
         )
-        interleave(a0_stage[:, 240:, :], a0_raw[:, :, 240:])
+        interleave(a0_stage[:, 192:, :], a0_raw[:, :, 192:])
         a0_q = quantize("a0", a0_stage[:].rearrange("p v j -> p (v j)"), V)
         for half in range(2):
             hidden(2, half)
-        a1_stage = sb.tile([P, V, PACK], BF16, name="a1_stage", align_bytes=64)
-        interleave(a1_stage[:, : V // 2, :], a1_raw[0][:])
-
         last = PACK - 1
-        first = early.tile([P, 2, V], F32, name="fetched_first", offset=0, align_bytes=64)
-        third = early.tile([P, V], F32, name="fetched_third", offset=4096, align_bytes=64)
+        first = early.tile([P, 2, V], F32, name="fetched_first", offset=2048)
+        third = early.tile([P, V], F32, name="fetched_third", offset=6144)
         fetched = [first[:, 0, :], first[:, 1, :], third[:]]
         for t in range(last):
             nc.vector.tensor_copy(fetched[t], h[t][:].indirect(pos_t[1][:]))
+        a1_stage = early.tile([P, V, PACK], BF16, name="a1_stage", offset=8192, align_bytes=64)
+        nc.gpsimd.tensor_scalar(
+            a1_stage[:, :96, :], a1_raw[0][:, :, :96].rearrange("p j v -> p v j"), 1.0, 0.0, MULT, ADD
+        )
+        interleave(a1_stage[:, 96:320, :], a1_raw[0][:, :, 96:])
 
-        first_terms = sb.tile([P, PACK, V], F32, name="first_terms")
-        second_a = sb.tile([P, PACK, V // 2], F32, name="second_a")
-        second_b = late_pool.tile([P, PACK, V // 2], F32, name="second_b", offset=0)
+        terms_a = [sb.tile([P, PACK, V // 2], F32, name=f"terms_a{d}") for d in range(D)]
+        terms_b = [
+            sb.tile([P, PACK, V // 2], F32, name="terms_b0"),
+            late_pool.tile([P, PACK, V // 2], F32, name="terms_b1", offset=0),
+        ]
 
         def term(d, tiles, cols):
-            if d == 0:
-                return first_terms[:, tiles, cols]
             if cols.stop <= V // 2:
-                return second_a[:, tiles, cols]
-            return second_b[:, tiles, cols.start - V // 2 : cols.stop - V // 2]
+                return terms_a[d][:, tiles, cols]
+            return terms_b[d][:, tiles, cols.start - V // 2 : cols.stop - V // 2]
 
         staged = sb.tile([P, PACK, V], F32, name="staged")
 
@@ -193,42 +195,50 @@ def tile_picked_dime_none_p_kernel(
         def psum_term(t, cols):
             nc.vector.tensor_tensor(term(1, t, cols), fetched[t][:, cols], late[t, cols.start // (V // 2)], MULT)
 
-        def stage_filter(d, t, a_q):
-            nc.scalar.copy(staged[:, t, :], filters(d, t, a_q)[:])
-            return staged[:, t, :]
-
-        whole = slice(0, V)
         for k, cols in enumerate((half_a, half_b)):
             acc = bank(k)
             product(acc[:, : V // 2], w3_q[0], slice(0, P), a0_q, cols)
             nc.scalar.copy(staged[:, 0, cols], acc[:, : V // 2])
             fused_term(0, 0, staged[:, 0, cols], cols)
-        fused_term(0, 1, stage_filter(0, 1, a0_q), whole)
-        interleave(a1_stage[:, V // 2 :, :], a1_raw[1][:])
+        bank01 = filters(0, 1, a0_q)
+        nc.scalar.copy(staged[:, 1, half_a], bank01[:, half_a])
+        fused_term(0, 1, staged[:, 1, half_a], half_a)
+        interleave(a1_stage[:, 320:, :], a1_raw[1][:])
         a1_q = quantize("a1", a1_stage[:].rearrange("p v j -> p (v j)"), V)
-        filt02 = stage_filter(0, 2, a0_q)
+        filt02 = staged[:, 2, :]
+        nc.scalar.copy(filt02, filters(0, 2, a0_q)[:])
         fused_term(0, 2, filt02[:, half_a], half_a)
         for half in range(2):
             hidden(last, half)
         bank03 = filters(0, last, a0_q)
         late = {}
-        for k, cols in enumerate((half_a, half_b)):
-            for u in range(2):
-                acc = bank(PACK + 2 * k + u)
-                for e in range(2):
-                    late[2 * u + e, k] = acc[:, e * (V // 2) : (e + 1) * (V // 2)]
-                    product(late[2 * u + e, k], w3_q[u], slice(e * P, (e + 1) * P), a1_q, cols)
-        filt03_a, filt13_a = staged[:, last, half_a], first_terms[:, 2, half_b]
+
+        def second_filter(t, k, acc):
+            late[t, k] = acc
+            product(acc, w3_q[t // 2], slice(t % 2 * P, (t % 2 + 1) * P), a1_q, (half_a, half_b)[k])
+
+        for t in range(2):
+            second_filter(t, 0, bank(PACK + t)[:, half_a])
+        acc = bank(3)
+        second_filter(2, 0, acc[:, half_a])
+        second_filter(last, 0, acc[:, half_b])
+        for u in range(2):
+            acc = bank(6 + u)
+            for e in range(2):
+                second_filter(2 * u + e, 1, acc[:, (half_a, half_b)[e]])
+        filt03_a, filt13_b = staged[:, last, half_a], staged[:, last, half_b]
+        filt13_a = terms_b[0][:].rearrange("p t v -> p (t v)")[:, 3 * P : 5 * P]
+        filt01_b = staged[:, 1, half_b]
         filt03_b = late_pool.tile([P, V // 2], F32, name="filt03_b", offset=0)
-        filt13_b = staged[:, last, half_b]
         nc.scalar.copy(filt03_a, bank03[:, half_a])
         nc.scalar.copy(filt13_a, late[last, 0])
+        nc.scalar.copy(filt01_b, bank01[:, half_b])
         nc.scalar.copy(filt03_b[:], bank03[:, half_b])
         nc.scalar.copy(filt13_b, late[last, 1])
 
         chunks = [slice(0, P), slice(P, 2 * P)]
         low_pair = bank(1)
-        back = bank(3)
+        back = bank(0)
 
         def add_on_tensor(acc, d, t, c):
             nc.tensor.matmul(acc, term(d, t, chunks[c]), ident[:], start=(d == 0), stop=(d == D - 1), is_transpose=True)
@@ -250,7 +260,7 @@ def tile_picked_dime_none_p_kernel(
                     add_on_tensor(low_pair[:, (2 * c + t) * P : (2 * c + t + 1) * P], d, t, c)
         fused_term(0, last, filt03_a, half_a)
         psum_term(2, half_a)
-        high_pair = [bank(2), bank(PACK)]
+        high_pair = [bank(PACK), bank(5)]
         for c in range(2):
             for d in range(D):
                 add_on_tensor(high_pair[c][:, :P], d, 2, c)
@@ -261,6 +271,7 @@ def tile_picked_dime_none_p_kernel(
         turn_back("turned_low", low_pair[:], [0, 2])
         for c in range(2):
             turn_back(f"turned_high{c}", high_pair[c][:, : 2 * P], [2 * c + 1])
+        fused_term(0, 1, filt01_b, half_b)
         fused_term(0, 2, filt02[:, half_b], half_b)
         fused_term(0, last, filt03_b[:], half_b)
         fused_term(1, last, filt13_b, half_b)
@@ -293,8 +304,8 @@ def tile_picked_dime_none_p_kernel(
             nc.scalar.dma_start(out[:, cols], result[:])
 
         parts = [slice(256, 384), slice(384, 512)]
-        project("z_a", z_a[:], half_a, 0)
+        project("z_a", z_a[:], half_a, 1)
         z_b0 = add_terms("z_b0", parts[0])
         z_b1 = add_terms("z_b1", parts[1])
-        project("z_b0", z_b0, parts[0], 1)
+        project("z_b0", z_b0, parts[0], 3)
         project("z_b1", z_b1, parts[1], 2)

@@ -148,28 +148,28 @@ def tile_picked_dime_none_p_kernel(
             for t in range(2):
                 hidden(t, half)
         w3_stage = [
-            deal_weight(f"w3_{u}", w3_raw, nc.vector.tensor_copy, u, 1, pool=early, offset=5120 * u) for u in range(2)
+            deal_weight(f"w3_{u}", w3_raw, nc.vector.tensor_copy, u, 1, pool=early, offset=1024 + 5120 * u) for u in range(2)
         ]
         w3_q = [quantize(f"w3_{u}", w3_stage[u][:], 2 * P) for u in range(2)]
         a0_stage = early.tile([P, V, PACK], BF16, name="a0_stage", offset=6144, align_bytes=64)
         nc.gpsimd.tensor_scalar(
-            a0_stage[:, :192, :], a0_raw[:, :, :192].rearrange("p j v -> p v j"), 1.0, 0.0, MULT, ADD
+            a0_stage[:, :256, :], a0_raw[:, :, :256].rearrange("p j v -> p v j"), 1.0, 0.0, MULT, ADD
         )
-        interleave(a0_stage[:, 192:, :], a0_raw[:, :, 192:])
+        interleave(a0_stage[:, 256:, :], a0_raw[:, :, 256:])
         a0_q = quantize("a0", a0_stage[:].rearrange("p v j -> p (v j)"), V)
         for half in range(2):
             hidden(2, half)
         last = PACK - 1
         first = early.tile([P, 2, V], F32, name="fetched_first", offset=2048)
-        third = early.tile([P, V], F32, name="fetched_third", offset=6144)
+        third = sb.tile([P, V], F32, name="fetched_third")
         fetched = [first[:, 0, :], first[:, 1, :], third[:]]
         for t in range(last):
             nc.vector.tensor_copy(fetched[t], h[t][:].indirect(pos_t[1][:]))
         a1_stage = early.tile([P, V, PACK], BF16, name="a1_stage", offset=8192, align_bytes=64)
         nc.gpsimd.tensor_scalar(
-            a1_stage[:, :96, :], a1_raw[0][:, :, :96].rearrange("p j v -> p v j"), 1.0, 0.0, MULT, ADD
+            a1_stage[:, :160, :], a1_raw[0][:, :, :160].rearrange("p j v -> p v j"), 1.0, 0.0, MULT, ADD
         )
-        interleave(a1_stage[:, 96:320, :], a1_raw[0][:, :, 96:])
+        interleave(a1_stage[:, 160:320, :], a1_raw[0][:, :, 160:])
 
         terms_a = [sb.tile([P, PACK, V // 2], F32, name=f"terms_a{d}") for d in range(D)]
         terms_b = [
@@ -294,18 +294,18 @@ def tile_picked_dime_none_p_kernel(
             )
             return z[:].rearrange("p v t -> p (v t)")
 
-        def project(name, z, cols, b):
+        def project(name, z, cols, b, copy, queue):
             width = cols.stop - cols.start
             z_q = quantize(name, z, width)
             acc = bank(b)
             product(acc[:, 0:width], (w2_codes, w2_plane), slice(0, N), z_q, slice(0, width))
             result = sb.tile([P, width], F32, name=name + "_result")
-            nc.scalar.copy(result[:], acc[:, 0:width])
-            nc.scalar.dma_start(out[:, cols], result[:])
+            copy(result[:], acc[:, 0:width])
+            queue.dma_start(out[:, cols], result[:])
 
         parts = [slice(256, 384), slice(384, 512)]
-        project("z_a", z_a[:], half_a, 1)
+        project("z_a", z_a[:], half_a, 1, nc.scalar.copy, nc.scalar)
         z_b0 = add_terms("z_b0", parts[0])
         z_b1 = add_terms("z_b1", parts[1])
-        project("z_b0", z_b0, parts[0], 3)
-        project("z_b1", z_b1, parts[1], 2)
+        project("z_b0", z_b0, parts[0], 3, nc.scalar.copy, nc.scalar)
+        project("z_b1", z_b1, parts[1], 2, nc.vector.tensor_copy, nc.sync)

@@ -203,6 +203,21 @@ def tile_picked_dime_none_p_kernel(
         bank01 = filters(0, 1, a0_q)
         nc.scalar.copy(staged[:, 1, half_a], bank01[:, half_a])
         fused_term(0, 1, staged[:, 1, half_a], half_a)
+        low_pair = bank(1)
+
+        def add_low_pair(d):
+            for t in range(2):
+                for c in range(2):
+                    nc.tensor.matmul(
+                        low_pair[:, (2 * c + t) * P : (2 * c + t + 1) * P],
+                        term(d, t, slice(c * P, (c + 1) * P)),
+                        ident[:],
+                        start=(d, t, c) == (0, 0, 0),
+                        stop=(d, t, c) == (1, 1, 1),
+                        is_transpose=True,
+                    )
+
+        add_low_pair(0)
         interleave(a1_stage[:, 320:, :], a1_raw[1][:])
         a1_q = quantize("a1", a1_stage[:].rearrange("p v j -> p (v j)"), V)
         filt02 = staged[:, 2, :]
@@ -237,7 +252,6 @@ def tile_picked_dime_none_p_kernel(
         nc.scalar.copy(filt13_b, late[last, 1])
 
         chunks = [slice(0, P), slice(P, 2 * P)]
-        low_pair = bank(1)
         back = bank(0)
 
         def add_on_tensor(acc, d, t, c):
@@ -254,10 +268,7 @@ def tile_picked_dime_none_p_kernel(
 
         psum_term(0, half_a)
         psum_term(1, half_a)
-        for c in range(2):
-            for t in range(2):
-                for d in range(D):
-                    add_on_tensor(low_pair[:, (2 * c + t) * P : (2 * c + t + 1) * P], d, t, c)
+        add_low_pair(1)
         fused_term(0, last, filt03_a, half_a)
         psum_term(2, half_a)
         high_pair = [bank(PACK), bank(5)]

@@ -118,10 +118,10 @@ def tile_picked_dime_none_p_kernel(
         h = [sb.tile([P, S], F32, name=f"h{t}") for t in range(2)]
         h += [middle.tile([P, S], F32, name=f"h{t}", offset=(t - 2) * 5120) for t in range(2, PACK)]
 
-        def hidden(t, half):
+        def hidden(t, half, b):
             codes, scales = w1_q[t // 2]
             cols = slice(t % 2 * P, (t % 2 + 1) * P)
-            acc = bank(2 * t + half)
+            acc = bank(b)
             nc.tensor.matmul_mx(
                 out=acc[:],
                 lhsT=codes[:, cols].bitcast(FP8X4),
@@ -139,14 +139,14 @@ def tile_picked_dime_none_p_kernel(
                 in_=raw.rearrange("p j (c i) -> p c j i", i=4),
             )
 
-        def filters(d, t, a_q):
-            acc = bank((t + 1) % PACK)
+        def filters(t, a_q, b):
+            acc = bank(b)
             product(acc[:], w3_q[t // 2], slice(t % 2 * P, (t % 2 + 1) * P), a_q, slice(0, V))
             return acc
 
         for half in range(2):
             for t in range(2):
-                hidden(t, half)
+                hidden(t, half, 2 * t + half)
         w3_stage = [
             deal_weight(f"w3_{u}", w3_raw, nc.vector.tensor_copy, u, 1, pool=early, offset=1024 + 5120 * u) for u in range(2)
         ]
@@ -158,7 +158,7 @@ def tile_picked_dime_none_p_kernel(
         interleave(a0_stage[:, 256:, :], a0_raw[:, :, 256:])
         a0_q = quantize("a0", a0_stage[:].rearrange("p v j -> p (v j)"), V)
         for half in range(2):
-            hidden(2, half)
+            hidden(2, half, 1 + 2 * half)
         last = PACK - 1
         first = early.tile([P, 2, V], F32, name="fetched_first", offset=2048)
         third = sb.tile([P, V], F32, name="fetched_third")
@@ -196,14 +196,14 @@ def tile_picked_dime_none_p_kernel(
             nc.vector.tensor_tensor(term(1, t, cols), fetched[t][:, cols], late[t, cols.start // (V // 2)], MULT)
 
         for k, cols in enumerate((half_a, half_b)):
-            acc = bank(k)
+            acc = bank(PACK * k)
             product(acc[:, : V // 2], w3_q[0], slice(0, P), a0_q, cols)
             nc.scalar.copy(staged[:, 0, cols], acc[:, : V // 2])
             fused_term(0, 0, staged[:, 0, cols], cols)
-        bank01 = filters(0, 1, a0_q)
+        bank01 = filters(1, a0_q, 2)
         nc.scalar.copy(staged[:, 1, half_a], bank01[:, half_a])
         fused_term(0, 1, staged[:, 1, half_a], half_a)
-        low_pair = bank(1)
+        low_pair = bank(4)
 
         def add_low_pair(d):
             for t in range(2):
@@ -221,11 +221,11 @@ def tile_picked_dime_none_p_kernel(
         interleave(a1_stage[:, 320:, :], a1_raw[1][:])
         a1_q = quantize("a1", a1_stage[:].rearrange("p v j -> p (v j)"), V)
         filt02 = staged[:, 2, :]
-        nc.scalar.copy(filt02, filters(0, 2, a0_q)[:])
+        nc.scalar.copy(filt02, filters(2, a0_q, 5)[:])
         fused_term(0, 2, filt02[:, half_a], half_a)
         for half in range(2):
-            hidden(last, half)
-        bank03 = filters(0, last, a0_q)
+            hidden(last, half, 1 - half)
+        bank03 = filters(last, a0_q, 6)
         late = {}
 
         def second_filter(t, k, acc):
@@ -233,12 +233,12 @@ def tile_picked_dime_none_p_kernel(
             product(acc, w3_q[t // 2], slice(t % 2 * P, (t % 2 + 1) * P), a1_q, (half_a, half_b)[k])
 
         for t in range(2):
-            second_filter(t, 0, bank(PACK + t)[:, half_a])
-        acc = bank(3)
+            second_filter(t, 0, bank((7, 3)[t])[:, half_a])
+        acc = bank(5)
         second_filter(2, 0, acc[:, half_a])
         second_filter(last, 0, acc[:, half_b])
         for u in range(2):
-            acc = bank(6 + u)
+            acc = bank(1 - u)
             for e in range(2):
                 second_filter(2 * u + e, 1, acc[:, (half_a, half_b)[e]])
         filt03_a, filt13_b = staged[:, last, half_a], staged[:, last, half_b]
@@ -252,10 +252,7 @@ def tile_picked_dime_none_p_kernel(
         nc.scalar.copy(filt13_b, late[last, 1])
 
         chunks = [slice(0, P), slice(P, 2 * P)]
-        back = bank(0)
-
-        def add_on_tensor(acc, d, t, c):
-            nc.tensor.matmul(acc, term(d, t, chunks[c]), ident[:], start=(d == 0), stop=(d == D - 1), is_transpose=True)
+        back = bank(6)
 
         def turn_back(name, sums, places):
             turned = sb.tile([P, len(places), 2 * P], BF16, name=name)
@@ -269,16 +266,26 @@ def tile_picked_dime_none_p_kernel(
         psum_term(0, half_a)
         psum_term(1, half_a)
         add_low_pair(1)
+        high_pair = [bank(7), bank(3)]
+
+        def add_high_pair(d, e):
+            for c in range(2):
+                nc.tensor.matmul(
+                    high_pair[c][:, e * P : (e + 1) * P],
+                    term(d, 2 + e, chunks[c]),
+                    ident[:],
+                    start=(d, e) == (0, 0),
+                    stop=(d, e) == (1, 1),
+                    is_transpose=True,
+                )
+
+        add_high_pair(0, 0)
         fused_term(0, last, filt03_a, half_a)
+        add_high_pair(0, 1)
         psum_term(2, half_a)
-        high_pair = [bank(PACK), bank(5)]
-        for c in range(2):
-            for d in range(D):
-                add_on_tensor(high_pair[c][:, :P], d, 2, c)
-            add_on_tensor(high_pair[c][:, P : 2 * P], 0, last, c)
+        add_high_pair(1, 0)
         fused_term(1, last, filt13_a, half_a)
-        for c in range(2):
-            add_on_tensor(high_pair[c][:, P : 2 * P], 1, last, c)
+        add_high_pair(1, 1)
         turn_back("turned_low", low_pair[:], [0, 2])
         for c in range(2):
             turn_back(f"turned_high{c}", high_pair[c][:, : 2 * P], [2 * c + 1])
@@ -315,8 +322,8 @@ def tile_picked_dime_none_p_kernel(
             queue.dma_start(out[:, cols], result[:])
 
         parts = [slice(256, 384), slice(384, 512)]
-        project("z_a", z_a[:], half_a, 1, nc.scalar.copy, nc.scalar)
+        project("z_a", z_a[:], half_a, 4, nc.scalar.copy, nc.scalar)
         z_b0 = add_terms("z_b0", parts[0])
         z_b1 = add_terms("z_b1", parts[1])
-        project("z_b0", z_b0, parts[0], 3, nc.scalar.copy, nc.scalar)
+        project("z_b0", z_b0, parts[0], 5, nc.scalar.copy, nc.scalar)
         project("z_b1", z_b1, parts[1], 2, nc.vector.tensor_copy, nc.sync)

@@ -227,6 +227,7 @@ def tile_picked_dime_none_p_kernel(
             hidden(last, half, 1 - half)
         bank03 = filters(last, a0_q, 6)
         late = {}
+        late_banks = {}
 
         def second_filter(t, k, acc):
             late[t, k] = acc
@@ -238,7 +239,7 @@ def tile_picked_dime_none_p_kernel(
         second_filter(2, 0, acc[:, half_a])
         second_filter(last, 0, acc[:, half_b])
         for u in range(2):
-            acc = bank(1 - u)
+            acc = late_banks[u] = bank(1 - u)
             for e in range(2):
                 second_filter(2 * u + e, 1, acc[:, (half_a, half_b)[e]])
         filt03_a, filt13_b = staged[:, last, half_a], staged[:, last, half_b]
@@ -293,14 +294,19 @@ def tile_picked_dime_none_p_kernel(
         fused_term(0, 2, filt02[:, half_b], half_b)
         fused_term(0, last, filt03_b[:], half_b)
         fused_term(1, last, filt13_b, half_b)
-        for t in range(last):
-            psum_term(t, half_b)
-
-        z_a = late_pool.tile([P, V // 2 * PACK], BF16, name="z_a", offset=4096, align_bytes=64)
-        nc.scalar.copy(
-            out=z_a[:].bitcast(F32).rearrange("p (c v u) -> p c v u", c=2, u=2),
-            in_=back[:].rearrange("p (c u v) -> p c v u", c=2, u=2),
+        nc.vector.tensor_tensor(
+            term(1, slice(0, 2), half_b), first[:, :, half_b], late_banks[0][:].rearrange("p (t v) -> p t v", t=2), MULT
         )
+        psum_term(2, half_b)
+
+        z_a = []
+        for c in range(2):
+            z = late_pool.tile([P, P * PACK], BF16, name=f"z_a{c}", offset=4096 + 1024 * c, align_bytes=64)
+            nc.scalar.copy(
+                out=z[:].bitcast(F32).rearrange("p (v u) -> p v u", u=2),
+                in_=back[:, 2 * c * P : 2 * (c + 1) * P].rearrange("p (u v) -> p v u", u=2),
+            )
+            z_a.append(z[:])
 
         def add_terms(name, cols):
             z = late_pool.tile([P, P, PACK], BF16, name=name, offset=4096 + 8 * (cols.start - V // 2), align_bytes=64)
@@ -312,9 +318,14 @@ def tile_picked_dime_none_p_kernel(
             )
             return z[:].rearrange("p v t -> p (v t)")
 
-        def project(name, z, cols, b, copy, queue):
+        def project(name, pieces, cols, b, copy, queue):
             width = cols.stop - cols.start
-            z_q = quantize(name, z, width)
+            z_q = (
+                sb.tile([P, width], U32, name=name + "_codes", align_bytes=64),
+                sb.tile([P, width], U8, name=name + "_scales", align_bytes=64),
+            )
+            for c, z in enumerate(pieces):
+                nc.vector.quantize_mx(out=z_q[0][:, chunks[c]].bitcast(FP8X4), scales=z_q[1][:, chunks[c]], in_=z)
             acc = bank(b)
             product(acc[:, 0:width], (w2_codes, w2_plane), slice(0, N), z_q, slice(0, width))
             result = sb.tile([P, width], F32, name=name + "_result")
@@ -322,8 +333,8 @@ def tile_picked_dime_none_p_kernel(
             queue.dma_start(out[:, cols], result[:])
 
         parts = [slice(256, 384), slice(384, 512)]
-        project("z_a", z_a[:], half_a, 4, nc.scalar.copy, nc.scalar)
+        project("z_a", z_a, half_a, 4, nc.scalar.copy, nc.scalar)
         z_b0 = add_terms("z_b0", parts[0])
         z_b1 = add_terms("z_b1", parts[1])
-        project("z_b0", z_b0, parts[0], 5, nc.scalar.copy, nc.scalar)
-        project("z_b1", z_b1, parts[1], 2, nc.vector.tensor_copy, nc.sync)
+        project("z_b0", [z_b0], parts[0], 5, nc.scalar.copy, nc.scalar)
+        project("z_b1", [z_b1], parts[1], 2, nc.vector.tensor_copy, nc.sync)

@@ -1,7 +1,6 @@
 from contextlib import ExitStack
 
 import concourse.mybir as mybir
-from concourse.masks import make_identity
 
 F32 = mybir.dt.float32
 BF16 = mybir.dt.bfloat16
@@ -13,6 +12,7 @@ FP8X4 = mybir.dt.float8_e4m3fn_x4
 MULT = mybir.AluOpType.mult
 ADD = mybir.AluOpType.add
 SILU = mybir.ActivationFunctionType.Silu
+COPY = mybir.ActivationFunctionType.Copy
 
 K, T, S, V, H, N, D = 512, 2048, 1024, 512, 512, 128, 2
 P = 128
@@ -32,18 +32,18 @@ def tile_picked_dime_none_p_kernel(
         def bank(b):
             return psum.tile([P, BANK], F32, name=f"bank{b}")
 
-        def load_scale_rows(plane, rows, queue=nc.sync):
+        def load_scale_rows(plane, rows):
             by_quadrant = rows[0].bitcast(I32).rearrange("(q r) c -> r q c", r=4)
             for r in range(4):
-                queue.dma_start(plane[r:P:32, :].bitcast(I32), by_quadrant[r])
+                nc.sync.dma_start(plane[r:P:32, :].bitcast(I32), by_quadrant[r])
 
         def load_rows(name, rows, pool=sb, **place):
             raw = pool.tile([P, PACK, rows.shape[1]], F32, name=name, **place)
             nc.sync.dma_start(raw[:], rows.rearrange("(p j) c -> p j c", j=PACK))
             return raw
 
-        def quantize(name, grouped, width, pool=sb, **place):
-            codes = pool.tile([P, width], U32, name=name + "_codes", align_bytes=64, **place)
+        def quantize(name, grouped, width):
+            codes = sb.tile([P, width], U32, name=name + "_codes", align_bytes=64)
             scales = sb.tile([P, width], U8, name=name + "_scales", align_bytes=64)
             nc.vector.quantize_mx(out=codes[:].bitcast(FP8X4), scales=scales[:], in_=grouped)
             return codes, scales
@@ -59,17 +59,21 @@ def tile_picked_dime_none_p_kernel(
                 stop=True,
             )
 
-        def deal_weight(name, raw, copy, pair0, pairs, pool=sb, **place):
-            grouped = pool.tile([P, pairs * 2 * P * PACK], BF16, name=name + "_bf16", align_bytes=64, **place)
+        def deal_weight(name, raw, copy, pair, pool=sb, **place):
+            grouped = pool.tile([P, 2 * P * PACK], BF16, name=name + "_bf16", align_bytes=64, **place)
             copy(
-                out=grouped[:].rearrange("p (u e m j) -> p u m j e", u=pairs, e=2, j=PACK),
-                in_=raw[:].rearrange("p j (m u e) -> p u m j e", u=2, e=2)[:, pair0 : pair0 + pairs],
+                out=grouped[:].rearrange("p (e m j) -> p m j e", e=2, j=PACK),
+                in_=raw[:].rearrange("p j (m u e) -> p u m j e", u=2, e=2)[:, pair],
             )
             return grouped
-        early = ctx.enter_context(tc.tile_pool(name="early", bufs=1))
-        late_pool = ctx.enter_context(tc.tile_pool(name="late", bufs=1))
-        middle = ctx.enter_context(tc.tile_pool(name="middle", bufs=1))
 
+        def interleave(copy, stage, raw):
+            copy(
+                out=stage.rearrange("p (c i) j -> p c j i", i=4),
+                in_=raw.rearrange("p j (c i) -> p c j i", i=4),
+            )
+
+        shared = ctx.enter_context(tc.tile_pool(name="shared", bufs=1))
         x_plane = sb.tile([P, T], U8, name="x_plane", align_bytes=64)
         nc.gpsimd.memset(x_plane[:].bitcast(I32), 0)
         warm = sb.tile([P, 2], F32, name="warm")
@@ -79,34 +83,28 @@ def tile_picked_dime_none_p_kernel(
         nc.sync.dma_start(offs_t[:], offs)
         w1_raw = sb.tile([P, PACK, H], F32, name="w1_raw")
         w1_src = w1.rearrange("(p j) c -> p j c", j=PACK)
-        nc.sync.dma_start(w1_raw[:, 0:1, :], w1_src[:, 0:1, :])
+        nc.sync.dma_start(w1_raw[:, 0:2, :], w1_src[:, 0:2, :])
         load_scale_rows(x_plane, x_scales)
-        nc.sync.dma_start(w1_raw[:, 1:PACK, :], w1_src[:, 1:PACK, :])
+        nc.sync.dma_start(w1_raw[:, 2:PACK, :], w1_src[:, 2:PACK, :])
         x_table = sb.tile([P, T], I32, name="x_table", align_bytes=64)
         nc.sync.dma_start(x_table[:], x_words[0].rearrange("p n t -> p (n t)").bitcast(I32))
         w3_raw = load_rows("w3_raw", w3)
         pos_t = [sb.tile([P, V // 16], U16, name=f"pos{d}_t") for d in range(D)]
-        nc.sync.dma_start(pos_t[1][:], pos2)
-        a0_raw = load_rows("a0_raw", aT[:, :V], pool=middle, offset=0)
         nc.sync.dma_start(pos_t[0][:], pos1)
-        a1_raw = [
-            load_rows("a1_raw0", aT[:, V : V + 320]),
-            load_rows("a1_raw1", aT[:, V + 320 :], pool=middle, offset=8192),
-        ]
+        a_raw = [load_rows("a0_raw", aT[:, :V])]
+        nc.sync.dma_start(pos_t[1][:], pos2)
+        a_raw.append(load_rows("a1_raw", aT[:, V:], pool=shared, offset=4096))
         w2_codes = sb.tile([P, N], I32, name="w2_codes", align_bytes=64)
         nc.sync.dma_start(w2_codes[:], w2_words[0].rearrange("p n t -> p (n t)").bitcast(I32))
         w2_plane = sb.tile([P, N], U8, name="w2_plane", align_bytes=64)
         nc.gpsimd.memset(w2_plane[:], 0)
         load_scale_rows(w2_plane, w2_scales)
 
-        ident = sb.tile([P, P], F32, name="ident")
-        make_identity(nc, ident[:])
-
         picked_scales = sb.tile([P, S], U8, name="picked_scales", align_bytes=64)
         nc.vector.tensor_copy(picked_scales[:], x_plane[:].indirect(offs_t[:]))
-        w1_low = deal_weight("w1_low", w1_raw, nc.scalar.copy, 0, 1)
-        w1_high = deal_weight("w1_high", w1_raw, nc.vector.tensor_copy, 1, 1)
-        w1_q = [quantize("w1_low", w1_low[:], 2 * P), quantize("w1_high", w1_high[:], 2 * P)]
+        w1_low = deal_weight("w1_low", w1_raw, nc.scalar.copy, 0, pool=shared, offset=0)
+        w1_q = [quantize("w1_low", w1_low[:], 2 * P)]
+        w1_high = deal_weight("w1_high", w1_raw, nc.scalar.copy, 1, pool=shared, offset=0)
         words = []
         for half in range(S // BANK):
             picked = sb.tile([P, BANK], U32, name=f"picked_words{half}", align_bytes=64)
@@ -114,227 +112,106 @@ def tile_picked_dime_none_p_kernel(
                 picked[:], x_table[:].bitcast(U32).indirect(offs_t[:, half * (BANK // 16) : (half + 1) * (BANK // 16)])
             )
             words.append(picked)
+            if half == 0:
+                w1_q.append(quantize("w1_high", w1_high[:], 2 * P))
 
-        h = [sb.tile([P, S], F32, name=f"h{t}") for t in range(2)]
-        h += [middle.tile([P, S], F32, name=f"h{t}", offset=(t - 2) * 5120) for t in range(2, PACK)]
-
-        def hidden(t, half, b):
-            codes, scales = w1_q[t // 2]
-            cols = slice(t % 2 * P, (t % 2 + 1) * P)
-            acc = bank(b)
-            nc.tensor.matmul_mx(
-                out=acc[:],
-                lhsT=codes[:, cols].bitcast(FP8X4),
-                lhsT_scale=scales[:, cols],
-                rhs=words[half][:].bitcast(FP8X4),
-                rhs_scale=picked_scales[:, half * BANK : (half + 1) * BANK],
-                start=True,
-                stop=True,
-            )
-            nc.scalar.activation(h[t][:, half * BANK : (half + 1) * BANK], acc[:], SILU)
-
-        def interleave(stage, raw):
-            nc.scalar.copy(
-                out=stage.rearrange("p (c i) j -> p c j i", i=4),
-                in_=raw.rearrange("p j (c i) -> p c j i", i=4),
-            )
-
-        def filters(t, a_q, b):
-            acc = bank(b)
-            product(acc[:], w3_q[t // 2], slice(t % 2 * P, (t % 2 + 1) * P), a_q, slice(0, V))
-            return acc
-
-        for half in range(2):
-            for t in range(2):
-                hidden(t, half, 2 * t + half)
-        w3_stage = [
-            deal_weight(f"w3_{u}", w3_raw, nc.vector.tensor_copy, u, 1, pool=early, offset=1024 + 5120 * u) for u in range(2)
-        ]
-        w3_q = [quantize(f"w3_{u}", w3_stage[u][:], 2 * P) for u in range(2)]
-        a0_stage = early.tile([P, V, PACK], BF16, name="a0_stage", offset=6144, align_bytes=64)
-        nc.gpsimd.tensor_scalar(
-            a0_stage[:, :256, :], a0_raw[:, :, :256].rearrange("p j v -> p v j"), 1.0, 0.0, MULT, ADD
-        )
-        interleave(a0_stage[:, 256:, :], a0_raw[:, :, 256:])
-        a0_q = quantize("a0", a0_stage[:].rearrange("p v j -> p (v j)"), V)
-        for half in range(2):
-            hidden(2, half, 1 + 2 * half)
-        last = PACK - 1
-        first = early.tile([P, 2, V], F32, name="fetched_first", offset=2048)
-        third = sb.tile([P, V], F32, name="fetched_third")
-        fetched = [first[:, 0, :], first[:, 1, :], third[:]]
-        for t in range(last):
-            nc.vector.tensor_copy(fetched[t], h[t][:].indirect(pos_t[1][:]))
-        a1_stage = early.tile([P, V, PACK], BF16, name="a1_stage", offset=8192, align_bytes=64)
-        nc.gpsimd.tensor_scalar(
-            a1_stage[:, :160, :], a1_raw[0][:, :, :160].rearrange("p j v -> p v j"), 1.0, 0.0, MULT, ADD
-        )
-        interleave(a1_stage[:, 160:320, :], a1_raw[0][:, :, 160:])
-
-        terms_a = [sb.tile([P, PACK, V // 2], F32, name=f"terms_a{d}") for d in range(D)]
-        terms_b = [
-            sb.tile([P, PACK, V // 2], F32, name="terms_b0"),
-            late_pool.tile([P, PACK, V // 2], F32, name="terms_b1", offset=0),
-        ]
-
-        def term(d, tiles, cols):
-            if cols.stop <= V // 2:
-                return terms_a[d][:, tiles, cols]
-            return terms_b[d][:, tiles, cols.start - V // 2 : cols.stop - V // 2]
-
-        staged = sb.tile([P, PACK, V], F32, name="staged")
-
-        half_a, half_b = slice(0, V // 2), slice(V // 2, V)
-
-        def offsets(d, cols):
-            return pos_t[d][:, cols.start // 16 : cols.stop // 16]
-
-        def fused_term(d, t, filt, cols):
-            nc.vector.tensor_tensor(term(d, t, cols), h[t][:].indirect(offsets(d, cols)), filt, MULT)
-
-        def psum_term(t, cols):
-            nc.vector.tensor_tensor(term(1, t, cols), fetched[t][:, cols], late[t, cols.start // (V // 2)], MULT)
-
-        for k, cols in enumerate((half_a, half_b)):
-            acc = bank(PACK * k)
-            product(acc[:, : V // 2], w3_q[0], slice(0, P), a0_q, cols)
-            nc.scalar.copy(staged[:, 0, cols], acc[:, : V // 2])
-            fused_term(0, 0, staged[:, 0, cols], cols)
-        bank01 = filters(1, a0_q, 2)
-        nc.scalar.copy(staged[:, 1, half_a], bank01[:, half_a])
-        fused_term(0, 1, staged[:, 1, half_a], half_a)
-        low_pair = bank(4)
-
-        def add_low_pair(d):
-            for t in range(2):
-                for c in range(2):
-                    nc.tensor.matmul(
-                        low_pair[:, (2 * c + t) * P : (2 * c + t + 1) * P],
-                        term(d, t, slice(c * P, (c + 1) * P)),
-                        ident[:],
-                        start=(d, t, c) == (0, 0, 0),
-                        stop=(d, t, c) == (1, 1, 1),
-                        is_transpose=True,
-                    )
-
-        add_low_pair(0)
-        interleave(a1_stage[:, 320:, :], a1_raw[1][:])
-        a1_q = quantize("a1", a1_stage[:].rearrange("p v j -> p (v j)"), V)
-        filt02 = staged[:, 2, :]
-        nc.scalar.copy(filt02, filters(2, a0_q, 5)[:])
-        fused_term(0, 2, filt02[:, half_a], half_a)
-        for half in range(2):
-            hidden(last, half, 1 - half)
-        bank03 = filters(last, a0_q, 6)
-        late = {}
-        late_banks = {}
-
-        def second_filter(t, k, acc):
-            late[t, k] = acc
-            product(acc, w3_q[t // 2], slice(t % 2 * P, (t % 2 + 1) * P), a1_q, (half_a, half_b)[k])
-
-        for t in range(2):
-            second_filter(t, 0, bank((7, 3)[t])[:, half_a])
-        acc = bank(5)
-        second_filter(2, 0, acc[:, half_a])
-        second_filter(last, 0, acc[:, half_b])
-        for u in range(2):
-            acc = late_banks[u] = bank(1 - u)
-            for e in range(2):
-                second_filter(2 * u + e, 1, acc[:, (half_a, half_b)[e]])
-        filt03_a, filt13_b = staged[:, last, half_a], staged[:, last, half_b]
-        filt13_a = terms_b[0][:].rearrange("p t v -> p (t v)")[:, 3 * P : 5 * P]
-        filt01_b = staged[:, 1, half_b]
-        filt03_b = late_pool.tile([P, V // 2], F32, name="filt03_b", offset=0)
-        nc.scalar.copy(filt03_a, bank03[:, half_a])
-        nc.scalar.copy(filt13_a, late[last, 0])
-        nc.scalar.copy(filt01_b, bank01[:, half_b])
-        nc.scalar.copy(filt03_b[:], bank03[:, half_b])
-        nc.scalar.copy(filt13_b, late[last, 1])
-
-        chunks = [slice(0, P), slice(P, 2 * P)]
-        back = bank(6)
-
-        def turn_back(name, sums, places):
-            turned = sb.tile([P, len(places), 2 * P], BF16, name=name)
-            nc.scalar.copy(
-                out=turned[:].rearrange("p c (q e) -> p c q e", e=2),
-                in_=sums.rearrange("p (c e q) -> p c q e", c=len(places), e=2),
-            )
-            for k, place in enumerate(places):
-                nc.tensor.transpose(back[:, place * P : (place + 1) * P], turned[:, k, :].bitcast(F32), ident[:])
-
-        psum_term(0, half_a)
-        psum_term(1, half_a)
-        add_low_pair(1)
-        high_pair = [bank(7), bank(3)]
-
-        def add_high_pair(d, e):
-            for c in range(2):
-                nc.tensor.matmul(
-                    high_pair[c][:, e * P : (e + 1) * P],
-                    term(d, 2 + e, chunks[c]),
-                    ident[:],
-                    start=(d, e) == (0, 0),
-                    stop=(d, e) == (1, 1),
-                    is_transpose=True,
+        h = [sb.tile([P, S], F32, name=f"h{t}") for t in range(PACK)]
+        for half in range(S // BANK):
+            cols = slice(half * BANK, (half + 1) * BANK)
+            for t in range(PACK):
+                acc = bank(PACK * half + t)
+                codes, scales = w1_q[t // 2]
+                rows = slice(t % 2 * P, (t % 2 + 1) * P)
+                nc.tensor.matmul_mx(
+                    out=acc[:],
+                    lhsT=codes[:, rows].bitcast(FP8X4),
+                    lhsT_scale=scales[:, rows],
+                    rhs=words[half][:].bitcast(FP8X4),
+                    rhs_scale=picked_scales[:, cols],
+                    start=True,
+                    stop=True,
                 )
+                nc.scalar.activation(h[t][:, cols], acc[:], SILU)
 
-        add_high_pair(0, 0)
-        fused_term(0, last, filt03_a, half_a)
-        add_high_pair(0, 1)
-        psum_term(2, half_a)
-        add_high_pair(1, 0)
-        fused_term(1, last, filt13_a, half_a)
-        add_high_pair(1, 1)
-        turn_back("turned_low", low_pair[:], [0, 2])
-        for c in range(2):
-            turn_back(f"turned_high{c}", high_pair[c][:, : 2 * P], [2 * c + 1])
-        fused_term(0, 1, filt01_b, half_b)
-        fused_term(0, 2, filt02[:, half_b], half_b)
-        fused_term(0, last, filt03_b[:], half_b)
-        fused_term(1, last, filt13_b, half_b)
-        nc.vector.tensor_tensor(
-            term(1, slice(0, 2), half_b), first[:, :, half_b], late_banks[0][:].rearrange("p (t v) -> p t v", t=2), MULT
-        )
-        psum_term(2, half_b)
+        w3_stage = [deal_weight(f"w3_{u}", w3_raw, nc.vector.tensor_copy, u) for u in range(2)]
+        w3_q = [quantize(f"w3_{u}", w3_stage[u][:], 2 * P) for u in range(2)]
+        a_q = []
+        for d in range(D):
+            stage = shared.tile([P, V, PACK], BF16, name=f"a{d}_stage", align_bytes=64, offset=12288 * d)
+            interleave(nc.vector.tensor_copy, stage[:], a_raw[d][:])
+            a_q.append(quantize(f"a{d}", stage[:].rearrange("p v j -> p (v j)"), V))
 
-        z_a = []
-        for c in range(2):
-            z = late_pool.tile([P, P * PACK], BF16, name=f"z_a{c}", offset=4096 + 1024 * c, align_bytes=64)
-            nc.scalar.copy(
-                out=z[:].bitcast(F32).rearrange("p (v u) -> p v u", u=2),
-                in_=back[:, 2 * c * P : 2 * (c + 1) * P].rearrange("p (u v) -> p v u", u=2),
-            )
-            z_a.append(z[:])
+        W = V // 2
+        halves = [slice(k * W, (k + 1) * W) for k in range(2)]
+        terms = {(k, d): sb.tile([P, PACK, W], F32, name=f"terms{k}{d}") for k, d in ((0, 0), (0, 1), (1, 1))}
+        terms[1, 0] = shared.tile([P, PACK, W], F32, name="terms10", offset=12288)
+        staged = {(k, 0, u): sb.tile([P, 2, W], F32, name=f"staged{k}0{u}") for k, u in ((0, 0), (1, 0), (1, 1))}
+        staged[0, 0, 1] = shared.tile([P, 2, W], F32, name="staged001", offset=0)
+        for k in range(2):
+            for u in range(2):
+                staged[k, 1, u] = shared.tile([P, 2, W], F32, name=f"staged{k}1{u}", offset=4096 + 2048 * (2 * k + u))
 
-        def add_terms(name, cols):
-            z = late_pool.tile([P, P, PACK], BF16, name=name, offset=4096 + 8 * (cols.start - V // 2), align_bytes=64)
+        def looked_up(k, d, t):
+            return h[t][:].indirect(pos_t[d][:, halves[k].start // 16 : halves[k].stop // 16])
+
+        def filters(k, d, u):
+            acc = bank(4 * k + 2 * d + u)
+            for e in range(2):
+                product(acc[:, e * W : (e + 1) * W], w3_q[u], slice(e * P, (e + 1) * P), a_q[d], halves[k])
+            return acc[:].rearrange("p (e v) -> p e v", e=2)
+
+        def fetch(k, d, u):
+            for t in (2 * u, 2 * u + 1):
+                nc.scalar.activation(staged[k, d, u][:, t % 2, :], looked_up(k, d, t), COPY)
+
+        def multiply(k, d, u):
+            pair = slice(2 * u, 2 * u + 2)
+            nc.vector.tensor_tensor(terms[k, d][:, pair, :], staged[k, d, u][:], filters(k, d, u), MULT)
+
+        def stage_filters(k, d, u):
+            nc.scalar.copy(staged[k, d, u][:], filters(k, d, u))
+
+        def fused(k, d, u):
+            for t in (2 * u, 2 * u + 1):
+                nc.vector.tensor_tensor(terms[k, d][:, t, :], looked_up(k, d, t), staged[k, d, u][:, t % 2, :], MULT)
+
+        def add_terms(name, k, cols):
+            z = sb.tile([P, cols.stop - cols.start, PACK], BF16, name=name, align_bytes=64)
             nc.vector.tensor_tensor(
                 z[:].rearrange("p (c i) t -> p c t i", i=4),
-                term(0, slice(0, PACK), cols).rearrange("p t (c i) -> p c t i", i=4),
-                term(1, slice(0, PACK), cols).rearrange("p t (c i) -> p c t i", i=4),
+                terms[k, 0][:, :, cols].rearrange("p t (c i) -> p c t i", i=4),
+                terms[k, 1][:, :, cols].rearrange("p t (c i) -> p c t i", i=4),
                 ADD,
             )
             return z[:].rearrange("p v t -> p (v t)")
 
-        def project(name, pieces, cols, b, copy, queue):
+        def project(name, z, cols, b, copy, queue):
             width = cols.stop - cols.start
-            z_q = (
-                sb.tile([P, width], U32, name=name + "_codes", align_bytes=64),
-                sb.tile([P, width], U8, name=name + "_scales", align_bytes=64),
-            )
-            for c, z in enumerate(pieces):
-                nc.vector.quantize_mx(out=z_q[0][:, chunks[c]].bitcast(FP8X4), scales=z_q[1][:, chunks[c]], in_=z)
+            z_q = quantize(name, z, width)
             acc = bank(b)
             product(acc[:, 0:width], (w2_codes, w2_plane), slice(0, N), z_q, slice(0, width))
             result = sb.tile([P, width], F32, name=name + "_result")
             copy(result[:], acc[:, 0:width])
             queue.dma_start(out[:, cols], result[:])
 
-        parts = [slice(256, 384), slice(384, 512)]
-        project("z_a", z_a, half_a, 4, nc.scalar.copy, nc.scalar)
-        z_b0 = add_terms("z_b0", parts[0])
-        z_b1 = add_terms("z_b1", parts[1])
-        project("z_b0", [z_b0], parts[0], 5, nc.scalar.copy, nc.scalar)
-        project("z_b1", [z_b1], parts[1], 2, nc.vector.tensor_copy, nc.sync)
+
+        fetch(0, 0, 0)
+        multiply(0, 0, 0)
+        stage_filters(1, 0, 0)
+        fused(1, 0, 0)
+        stage_filters(1, 0, 1)
+        fetch(0, 0, 1)
+        multiply(0, 0, 1)
+        fused(1, 0, 1)
+        for u in range(2):
+            fetch(0, 1, u)
+            multiply(0, 1, u)
+        z_a = add_terms("z_a", 0, slice(0, W))
+        fetch(1, 1, 0)
+        multiply(1, 1, 0)
+        fetch(1, 1, 1)
+        project("z_a", z_a, slice(0, W), 0, nc.scalar.copy, nc.sync)
+        multiply(1, 1, 1)
+        z_b = [add_terms(f"z_b{c}", 1, slice(c * P, (c + 1) * P)) for c in range(2)]
+        project("z_b0", z_b[0], slice(W, W + P), 1, nc.scalar.copy, nc.scalar)
+        project("z_b1", z_b[1], slice(W + P, V), 2, nc.vector.tensor_copy, nc.sync)

@@ -42,8 +42,8 @@ def tile_picked_dime_none_p_kernel(
             nc.sync.dma_start(raw[:], rows.rearrange("(p j) c -> p j c", j=PACK))
             return raw
 
-        def quantize(name, grouped, width):
-            codes = sb.tile([P, width], U32, name=name + "_codes", align_bytes=64)
+        def quantize(name, grouped, width, pool=sb, **place):
+            codes = pool.tile([P, width], U32, name=name + "_codes", align_bytes=64, **place)
             scales = sb.tile([P, width], U8, name=name + "_scales", align_bytes=64)
             nc.vector.quantize_mx(out=codes[:].bitcast(FP8X4), scales=scales[:], in_=grouped)
             return codes, scales
@@ -105,82 +105,84 @@ def tile_picked_dime_none_p_kernel(
         w1_low = deal_weight("w1_low", w1_raw, nc.scalar.copy, 0, pool=shared, offset=0)
         w1_q = [quantize("w1_low", w1_low[:], 2 * P)]
         w1_high = deal_weight("w1_high", w1_raw, nc.scalar.copy, 1, pool=shared, offset=0)
-        words = []
-        for half in range(S // BANK):
-            picked = sb.tile([P, BANK], U32, name=f"picked_words{half}", align_bytes=64)
+        pieces = [slice(0, 256), slice(256, 512), slice(512, S)]
+        words = [sb.tile([P, BANK], U32, name=f"picked_words{half}", align_bytes=64) for half in range(2)]
+
+        def pick_words(cols):
+            start = cols.start % BANK
             nc.vector.tensor_copy(
-                picked[:], x_table[:].bitcast(U32).indirect(offs_t[:, half * (BANK // 16) : (half + 1) * (BANK // 16)])
+                words[cols.start // BANK][:, start : start + cols.stop - cols.start],
+                x_table[:].bitcast(U32).indirect(offs_t[:, cols.start // 16 : cols.stop // 16]),
             )
-            words.append(picked)
-            if half == 0:
-                w1_q.append(quantize("w1_high", w1_high[:], 2 * P))
 
         h = [sb.tile([P, S], F32, name=f"h{t}") for t in range(PACK)]
-        for half in range(S // BANK):
-            cols = slice(half * BANK, (half + 1) * BANK)
-            for t in range(PACK):
-                acc = bank(PACK * half + t)
-                codes, scales = w1_q[t // 2]
-                rows = slice(t % 2 * P, (t % 2 + 1) * P)
-                nc.tensor.matmul_mx(
-                    out=acc[:],
-                    lhsT=codes[:, rows].bitcast(FP8X4),
-                    lhsT_scale=scales[:, rows],
-                    rhs=words[half][:].bitcast(FP8X4),
-                    rhs_scale=picked_scales[:, cols],
-                    start=True,
-                    stop=True,
-                )
-                nc.scalar.activation(h[t][:, cols], acc[:], SILU)
+
+        def hidden(t, cols, b):
+            acc = bank(b)
+            codes, scales = w1_q[t // 2]
+            rows = slice(t % 2 * P, (t % 2 + 1) * P)
+            width, start = cols.stop - cols.start, cols.start % BANK
+            nc.tensor.matmul_mx(
+                out=acc[:, :width],
+                lhsT=codes[:, rows].bitcast(FP8X4),
+                lhsT_scale=scales[:, rows],
+                rhs=words[cols.start // BANK][:, start : start + width].bitcast(FP8X4),
+                rhs_scale=picked_scales[:, cols],
+                start=True,
+                stop=True,
+            )
+            nc.scalar.activation(h[t][:, cols], acc[:, :width], SILU)
+
+        pick_words(pieces[0])
+        pick_words(pieces[1])
+        w1_q.append(quantize("w1_high", w1_high[:], 2 * P))
+        pick_words(pieces[2])
+        for k in range(2):
+            for t in range(2):
+                hidden(t, pieces[k], 2 * k + t)
+        for t in range(2, PACK):
+            hidden(t, slice(0, BANK), 2 + t)
+        for t in range(PACK):
+            hidden(t, pieces[2], (6 + t) % 8)
 
         w3_stage = [deal_weight(f"w3_{u}", w3_raw, nc.vector.tensor_copy, u) for u in range(2)]
         w3_q = [quantize(f"w3_{u}", w3_stage[u][:], 2 * P) for u in range(2)]
-        a_q = []
+        first, second, third = slice(0, 256), slice(256, 384), slice(384, V)
+        rest = slice(second.start, V)
+        a_q = {}
         for d in range(D):
-            stage = shared.tile([P, V, PACK], BF16, name=f"a{d}_stage", align_bytes=64, offset=12288 * d)
-            interleave(nc.vector.tensor_copy, stage[:], a_raw[d][:])
-            a_q.append(quantize(f"a{d}", stage[:].rearrange("p v j -> p (v j)"), V))
+            stages = [sb.tile([P, 256, PACK], BF16, name=f"a{d}_stage{k}", align_bytes=64) for k in range(2)]
+            for k, cols in enumerate((first, rest)):
+                interleave(nc.vector.tensor_copy, stages[k][:], a_raw[d][:, :, cols])
+            for k in range(2):
+                place = dict(pool=shared, offset=2048) if (d, k) == (0, 0) else {}
+                a_q[d, k] = quantize(f"a{d}_{k}", stages[k][:].rearrange("p v j -> p (v j)"), 256, **place)
 
-        W = V // 2
-        halves = [slice(k * W, (k + 1) * W) for k in range(2)]
-        terms = {(k, d): sb.tile([P, PACK, W], F32, name=f"terms{k}{d}") for k, d in ((0, 0), (0, 1), (1, 1))}
-        terms[1, 0] = shared.tile([P, PACK, W], F32, name="terms10", offset=12288)
-        staged = {(k, 0, u): sb.tile([P, 2, W], F32, name=f"staged{k}0{u}") for k, u in ((0, 0), (1, 0), (1, 1))}
-        staged[0, 0, 1] = shared.tile([P, 2, W], F32, name="staged001", offset=0)
-        for k in range(2):
-            for u in range(2):
-                staged[k, 1, u] = shared.tile([P, 2, W], F32, name=f"staged{k}1{u}", offset=4096 + 2048 * (2 * k + u))
+        def looked_up(d, t, cols):
+            return h[t][:].indirect(pos_t[d][:, cols.start // 16 : cols.stop // 16])
 
-        def looked_up(k, d, t):
-            return h[t][:].indirect(pos_t[d][:, halves[k].start // 16 : halves[k].stop // 16])
+        def filters(d, tiles, cols, b):
+            width = cols.stop - cols.start
+            acc = bank(b)
+            for e, t in enumerate(tiles):
+                product(acc[:, e * width : (e + 1) * width], w3_q[t // 2], slice(t % 2 * P, (t % 2 + 1) * P), a_q[d, cols.start // 256], slice(cols.start % 256, cols.start % 256 + width))
+            return acc[:].rearrange("p (e v) -> p e v", v=width)
 
-        def filters(k, d, u):
-            acc = bank(4 * k + 2 * d + u)
-            for e in range(2):
-                product(acc[:, e * W : (e + 1) * W], w3_q[u], slice(e * P, (e + 1) * P), a_q[d], halves[k])
-            return acc[:].rearrange("p (e v) -> p e v", e=2)
+        def fetch(name, d, tiles, cols, offset):
+            fetched = shared.tile([P, len(tiles), cols.stop - cols.start], F32, name=name, offset=offset)
+            for e, t in enumerate(tiles):
+                nc.scalar.activation(fetched[:, e, :], looked_up(d, t, cols), COPY)
+            return fetched
 
-        def fetch(k, d, u):
-            for t in (2 * u, 2 * u + 1):
-                nc.scalar.activation(staged[k, d, u][:, t % 2, :], looked_up(k, d, t), COPY)
+        def multiply(terms, fetched, d, tiles, cols, b):
+            nc.vector.tensor_tensor(terms[:, tiles[0] : tiles[-1] + 1, :], fetched[:], filters(d, tiles, cols, b), MULT)
 
-        def multiply(k, d, u):
-            pair = slice(2 * u, 2 * u + 2)
-            nc.vector.tensor_tensor(terms[k, d][:, pair, :], staged[k, d, u][:], filters(k, d, u), MULT)
-
-        def stage_filters(k, d, u):
-            nc.scalar.copy(staged[k, d, u][:], filters(k, d, u))
-
-        def fused(k, d, u):
-            for t in (2 * u, 2 * u + 1):
-                nc.vector.tensor_tensor(terms[k, d][:, t, :], looked_up(k, d, t), staged[k, d, u][:, t % 2, :], MULT)
-
-        def add_terms(name, k, cols):
-            z = sb.tile([P, cols.stop - cols.start, PACK], BF16, name=name, align_bytes=64)
+        def add_terms(name, terms0, terms1):
+            z = sb.tile([P, terms0.shape[2], PACK], BF16, name=name, align_bytes=64)
             nc.vector.tensor_tensor(
                 z[:].rearrange("p (c i) t -> p c t i", i=4),
-                terms[k, 0][:, :, cols].rearrange("p t (c i) -> p c t i", i=4),
-                terms[k, 1][:, :, cols].rearrange("p t (c i) -> p c t i", i=4),
+                terms0.rearrange("p t (c i) -> p c t i", i=4),
+                terms1.rearrange("p t (c i) -> p c t i", i=4),
                 ADD,
             )
             return z[:].rearrange("p v t -> p (v t)")
@@ -194,24 +196,27 @@ def tile_picked_dime_none_p_kernel(
             copy(result[:], acc[:, 0:width])
             queue.dma_start(out[:, cols], result[:])
 
+        low, high, every = [0, 1], [2, 3], [0, 1, 2, 3]
+        first0 = shared.tile([P, PACK, 256], F32, name="first0", offset=4096)
+        first1 = sb.tile([P, PACK, 256], F32, name="first1")
+        rest0 = sb.tile([P, PACK, 256], F32, name="rest0")
+        second1 = sb.tile([P, PACK, P], F32, name="second1")
+        third1 = sb.tile([P, PACK, P], F32, name="third1")
 
-        fetch(0, 0, 0)
-        multiply(0, 0, 0)
-        stage_filters(1, 0, 0)
-        fused(1, 0, 0)
-        stage_filters(1, 0, 1)
-        fetch(0, 0, 1)
-        multiply(0, 0, 1)
-        fused(1, 0, 1)
-        for u in range(2):
-            fetch(0, 1, u)
-            multiply(0, 1, u)
-        z_a = add_terms("z_a", 0, slice(0, W))
-        fetch(1, 1, 0)
-        multiply(1, 1, 0)
-        fetch(1, 1, 1)
-        project("z_a", z_a, slice(0, W), 0, nc.scalar.copy, nc.sync)
-        multiply(1, 1, 1)
-        z_b = [add_terms(f"z_b{c}", 1, slice(c * P, (c + 1) * P)) for c in range(2)]
-        project("z_b0", z_b[0], slice(W, W + P), 1, nc.scalar.copy, nc.scalar)
-        project("z_b1", z_b[1], slice(W + P, V), 2, nc.vector.tensor_copy, nc.sync)
+        staged = sb.tile([P, PACK, 256], F32, name="staged")
+        for u, tiles in enumerate((low, high)):
+            nc.scalar.copy(staged[:, 2 * u : 2 * u + 2, :], filters(0, tiles, first, 2 + u))
+        for t in every:
+            nc.vector.tensor_tensor(first0[:, t, :], looked_up(0, t, first), staged[:, t, :], MULT)
+        multiply(first1, fetch("got_first1_low", 1, low, first, 2048), 1, low, first, 6)
+        multiply(first1, fetch("got_first1_high", 1, high, first, 8192), 1, high, first, 7)
+        multiply(rest0, fetch("got_rest0_low", 0, low, rest, 10240), 0, low, rest, 4)
+        z_first = add_terms("z_first", first0[:], first1[:])
+        multiply(rest0, fetch("got_rest0_high", 0, high, rest, 2048), 0, high, rest, 5)
+        multiply(second1, fetch("got_second1", 1, every, second, 8192), 1, every, second, 0)
+        fetched = fetch("got_third1", 1, every, third, 10240)
+        project("z_first", z_first, first, 2, nc.scalar.copy, nc.sync)
+        z_second = add_terms("z_second", rest0[:, :, :P], second1[:])
+        multiply(third1, fetched, 1, every, third, 1)
+        project("z_second", z_second, second, 3, nc.scalar.copy, nc.scalar)
+        project("z_third", add_terms("z_third", rest0[:, :, P:], third1[:]), third, 4, nc.vector.tensor_copy, nc.sync)

@@ -91,8 +91,8 @@ def tile_picked_dime_none_p_kernel(
         w3_raw = load_rows("w3_raw", w3)
         pos_t = [sb.tile([P, V // 16], U16, name=f"pos{d}_t") for d in range(D)]
         nc.sync.dma_start(pos_t[0][:], pos1)
-        a_raw = [load_rows("a0_raw", aT[:, :V])]
         nc.sync.dma_start(pos_t[1][:], pos2)
+        a_raw = [load_rows("a0_raw", aT[:, :V], pool=shared, offset=12288)]
         a_raw.append(load_rows("a1_raw", aT[:, V:], pool=shared, offset=4096))
         w2_codes = sb.tile([P, N], I32, name="w2_codes", align_bytes=64)
         nc.sync.dma_start(w2_codes[:], w2_words[0].rearrange("p n t -> p (n t)").bitcast(I32))
@@ -149,17 +149,21 @@ def tile_picked_dime_none_p_kernel(
         w3_q = [quantize(f"w3_{u}", w3_stage[u][:], 2 * P) for u in range(2)]
         first, second, third = slice(0, 256), slice(256, 384), slice(384, V)
         rest = slice(second.start, V)
+
+        def looked_up(d, t, cols):
+            return h[t][:].indirect(pos_t[d][:, cols.start // 16 : cols.stop // 16])
+
         a_q = {}
         for d in range(D):
             stages = [sb.tile([P, 256, PACK], BF16, name=f"a{d}_stage{k}", align_bytes=64) for k in range(2)]
             for k, cols in enumerate((first, rest)):
                 interleave(nc.vector.tensor_copy, stages[k][:], a_raw[d][:, :, cols])
             for k in range(2):
-                place = dict(pool=shared, offset=2048) if (d, k) == (0, 0) else {}
-                a_q[d, k] = quantize(f"a{d}_{k}", stages[k][:].rearrange("p v j -> p (v j)"), 256, **place)
-
-        def looked_up(d, t, cols):
-            return h[t][:].indirect(pos_t[d][:, cols.start // 16 : cols.stop // 16])
+                a_q[d, k] = quantize(f"a{d}_{k}", stages[k][:].rearrange("p v j -> p (v j)"), 256)
+            if d == 0:
+                got_early = shared.tile([P, 2, 256], F32, name="got_early", offset=12288)
+                for t in range(2):
+                    nc.vector.tensor_copy(got_early[:, t, :], looked_up(0, t, first))
 
         def filters(d, tiles, cols, b):
             width = cols.stop - cols.start
@@ -168,14 +172,13 @@ def tile_picked_dime_none_p_kernel(
                 product(acc[:, e * width : (e + 1) * width], w3_q[t // 2], slice(t % 2 * P, (t % 2 + 1) * P), a_q[d, cols.start // 256], slice(cols.start % 256, cols.start % 256 + width))
             return acc[:].rearrange("p (e v) -> p e v", v=width)
 
-        def fetch(name, d, tiles, cols, offset):
-            fetched = shared.tile([P, len(tiles), cols.stop - cols.start], F32, name=name, offset=offset)
-            for e, t in enumerate(tiles):
-                nc.scalar.activation(fetched[:, e, :], looked_up(d, t, cols), COPY)
-            return fetched
+        def fetch(got, d, tiles, cols, start):
+            for t in tiles:
+                nc.scalar.activation(got[:, t, cols.start - start : cols.stop - start], looked_up(d, t, cols), COPY)
 
-        def multiply(terms, fetched, d, tiles, cols, b):
-            nc.vector.tensor_tensor(terms[:, tiles[0] : tiles[-1] + 1, :], fetched[:], filters(d, tiles, cols, b), MULT)
+        def multiply(terms, got, d, tiles, cols, b):
+            part = slice(tiles[0], tiles[-1] + 1)
+            nc.vector.tensor_tensor(terms[:, part, :], got[:, part, :], filters(d, tiles, cols, b), MULT)
 
         def add_terms(name, terms0, terms1):
             z = sb.tile([P, terms0.shape[2], PACK], BF16, name=name, align_bytes=64)
@@ -199,24 +202,32 @@ def tile_picked_dime_none_p_kernel(
         low, high, every = [0, 1], [2, 3], [0, 1, 2, 3]
         first0 = shared.tile([P, PACK, 256], F32, name="first0", offset=4096)
         first1 = sb.tile([P, PACK, 256], F32, name="first1")
-        rest0 = sb.tile([P, PACK, 256], F32, name="rest0")
+        rest0 = shared.tile([P, PACK, 256], F32, name="rest0", offset=20480)
         second1 = sb.tile([P, PACK, P], F32, name="second1")
         third1 = sb.tile([P, PACK, P], F32, name="third1")
+        got_first0 = sb.tile([P, PACK, 256], F32, name="got_first0")
+        got_rest0 = sb.tile([P, PACK, 256], F32, name="got_rest0")
+        got_first1_low = shared.tile([P, 2, 256], F32, name="got_first1_low", offset=20480)
+        got_first1 = sb.tile([P, PACK, 256], F32, name="got_first1")
+        got_second1 = sb.tile([P, PACK, P], F32, name="got_second1")
+        got_third1 = sb.tile([P, PACK, P], F32, name="got_third1")
 
-        staged = sb.tile([P, PACK, 256], F32, name="staged")
-        for u, tiles in enumerate((low, high)):
-            nc.scalar.copy(staged[:, 2 * u : 2 * u + 2, :], filters(0, tiles, first, 2 + u))
-        for t in every:
-            nc.vector.tensor_tensor(first0[:, t, :], looked_up(0, t, first), staged[:, t, :], MULT)
-        multiply(first1, fetch("got_first1_low", 1, low, first, 2048), 1, low, first, 6)
-        multiply(first1, fetch("got_first1_high", 1, high, first, 8192), 1, high, first, 7)
-        multiply(rest0, fetch("got_rest0_low", 0, low, rest, 10240), 0, low, rest, 4)
+        fetch(got_first0, 0, high, first, 0)
+        fetch(got_first1_low, 1, low, first, 0)
+        fetch(got_first1, 1, high, first, 0)
+        fetch(got_rest0, 0, every, rest, rest.start)
+        fetch(got_second1, 1, every, second, second.start)
+        fetch(got_third1, 1, every, third, third.start)
+        multiply(first0, got_early, 0, low, first, 2)
+        multiply(first0, got_first0, 0, high, first, 3)
+        multiply(first1, got_first1_low, 1, low, first, 6)
+        multiply(first1, got_first1, 1, high, first, 7)
+        multiply(rest0, got_rest0, 0, low, rest, 4)
         z_first = add_terms("z_first", first0[:], first1[:])
-        multiply(rest0, fetch("got_rest0_high", 0, high, rest, 2048), 0, high, rest, 5)
-        multiply(second1, fetch("got_second1", 1, every, second, 8192), 1, every, second, 0)
-        fetched = fetch("got_third1", 1, every, third, 10240)
+        multiply(rest0, got_rest0, 0, high, rest, 5)
+        multiply(second1, got_second1, 1, every, second, 0)
         project("z_first", z_first, first, 2, nc.scalar.copy, nc.sync)
         z_second = add_terms("z_second", rest0[:, :, :P], second1[:])
-        multiply(third1, fetched, 1, every, third, 1)
+        multiply(third1, got_third1, 1, every, third, 1)
         project("z_second", z_second, second, 3, nc.scalar.copy, nc.scalar)
         project("z_third", add_terms("z_third", rest0[:, :, P:], third1[:]), third, 4, nc.vector.tensor_copy, nc.sync)

@@ -161,8 +161,8 @@ def tile_picked_dime_none_p_kernel(
             for k in range(2):
                 a_q[d, k] = quantize(f"a{d}_{k}", stages[k][:].rearrange("p v j -> p (v j)"), 256)
             if d == 0:
-                got_early = shared.tile([P, 2, 256], F32, name="got_early", offset=12288)
-                for t in range(2):
+                got_early = shared.tile([P, 3, 256], F32, name="got_early", offset=12288)
+                for t in range(3):
                     nc.vector.tensor_copy(got_early[:, t, :], looked_up(0, t, first))
 
         def filters(d, tiles, cols, b):
@@ -212,14 +212,16 @@ def tile_picked_dime_none_p_kernel(
         got_second1 = sb.tile([P, PACK, P], F32, name="got_second1")
         got_third1 = sb.tile([P, PACK, P], F32, name="got_third1")
 
-        fetch(got_first0, 0, high, first, 0)
+        fetch(got_first0, 0, [3], first, 0)
         fetch(got_first1_low, 1, low, first, 0)
         fetch(got_first1, 1, high, first, 0)
         fetch(got_rest0, 0, every, rest, rest.start)
         fetch(got_second1, 1, every, second, second.start)
         fetch(got_third1, 1, every, third, third.start)
         multiply(first0, got_early, 0, low, first, 2)
-        multiply(first0, got_first0, 0, high, first, 3)
+        high_filters = filters(0, high, first, 3)
+        for e, got in enumerate((got_early, got_first0)):
+            nc.vector.tensor_tensor(first0[:, 2 + e, :], got[:, 2 + e, :], high_filters[:, e, :], MULT)
         multiply(first1, got_first1_low, 1, low, first, 6)
         multiply(first1, got_first1, 1, high, first, 7)
         multiply(rest0, got_rest0, 0, low, rest, 4)

from contextlib import ExitStack

import concourse.mybir as mybir

F32 = mybir.dt.float32
BF16 = mybir.dt.bfloat16
I32 = mybir.dt.int32
U32 = mybir.dt.uint32
U16 = mybir.dt.uint16
U8 = mybir.dt.uint8
FP8X4 = mybir.dt.float8_e4m3fn_x4
MULT = mybir.AluOpType.mult
ADD = mybir.AluOpType.add
SILU = mybir.ActivationFunctionType.Silu
COPY = mybir.ActivationFunctionType.Copy

K, T, S, V, H, N, D = 512, 2048, 1024, 512, 512, 128, 2
P = 128
PACK = 4
BANK = 512
FLOPS = 2 * K * H * S + 2 * K * H * D * V + 2 * H * N * V


def tile_picked_dime_none_p_kernel(
    tc, x_words, x_scales, aT, w1, w3, w2_words, w2_scales, offs, pos1, pos2, out
):
    nc = tc.nc
    with ExitStack() as ctx:
        sb = ctx.enter_context(tc.tile_pool(name="sb", bufs=1))
        psum = ctx.enter_context(tc.psum_pool(name="psum", bufs=1))

        def bank(b):
            return psum.tile([P, BANK], F32, name=f"bank{b}")

        def load_scale_rows(plane, rows):
            by_quadrant = rows[0].bitcast(I32).rearrange("(q r) c -> r q c", r=4)
            for r in range(4):
                nc.sync.dma_start(plane[r:P:32, :].bitcast(I32), by_quadrant[r])

        def load_rows(name, rows, pool=sb, **place):
            raw = pool.tile([P, PACK, rows.shape[1]], F32, name=name, **place)
            nc.sync.dma_start(raw[:], rows.rearrange("(p j) c -> p j c", j=PACK))
            return raw

        def quantize(name, grouped, width, pool=sb, **place):
            codes = pool.tile([P, width], U32, name=name + "_codes", align_bytes=64, **place)
            scales = sb.tile([P, width], U8, name=name + "_scales", align_bytes=64)
            nc.vector.quantize_mx(out=codes[:].bitcast(FP8X4), scales=scales[:], in_=grouped)
            return codes, scales

        def product(acc, stat, stat_cols, mov, mov_cols):
            nc.tensor.matmul_mx(
                out=acc,
                lhsT=stat[0][:, stat_cols].bitcast(FP8X4),
                lhsT_scale=stat[1][:, stat_cols],
                rhs=mov[0][:, mov_cols].bitcast(FP8X4),
                rhs_scale=mov[1][:, mov_cols],
                start=True,
                stop=True,
            )

        def deal_weight(name, raw, copy, pair, pool=sb, **place):
            grouped = pool.tile([P, 2 * P * PACK], BF16, name=name + "_bf16", align_bytes=64, **place)
            copy(
                out=grouped[:].rearrange("p (e m j) -> p m j e", e=2, j=PACK),
                in_=raw[:].rearrange("p j (m u e) -> p u m j e", u=2, e=2)[:, pair],
            )
            return grouped

        def interleave(copy, stage, raw):
            copy(
                out=stage.rearrange("p (c i) j -> p c j i", i=4),
                in_=raw.rearrange("p j (c i) -> p c j i", i=4),
            )

        shared = ctx.enter_context(tc.tile_pool(name="shared", bufs=1))
        x_plane = sb.tile([P, T], U8, name="x_plane", align_bytes=64)
        nc.gpsimd.memset(x_plane[:].bitcast(I32), 0)
        warm = sb.tile([P, 2], F32, name="warm")
        nc.vector.memset(warm[:, 0:1], 0.0)
        nc.scalar.activation(warm[:, 1:2], warm[:, 0:1], SILU)
        offs_t = sb.tile([P, S // 16], U16, name="offs_t")
        nc.sync.dma_start(offs_t[:], offs)
        w1_raw = sb.tile([P, PACK, H], F32, name="w1_raw")
        w1_src = w1.rearrange("(p j) c -> p j c", j=PACK)
        nc.sync.dma_start(w1_raw[:, 0:2, :], w1_src[:, 0:2, :])
        load_scale_rows(x_plane, x_scales)
        nc.sync.dma_start(w1_raw[:, 2:PACK, :], w1_src[:, 2:PACK, :])
        x_table = sb.tile([P, T], I32, name="x_table", align_bytes=64)
        nc.sync.dma_start(x_table[:], x_words[0].rearrange("p n t -> p (n t)").bitcast(I32))
        w3_raw = load_rows("w3_raw", w3)
        pos_t = [sb.tile([P, V // 16], U16, name=f"pos{d}_t") for d in range(D)]
        nc.sync.dma_start(pos_t[0][:], pos1)
        nc.sync.dma_start(pos_t[1][:], pos2)
        a_raw = [load_rows("a0_raw", aT[:, :V], pool=shared, offset=12288)]
        a_raw.append(load_rows("a1_raw", aT[:, V:], pool=shared, offset=4096))
        w2_codes = sb.tile([P, N], I32, name="w2_codes", align_bytes=64)
        nc.sync.dma_start(w2_codes[:], w2_words[0].rearrange("p n t -> p (n t)").bitcast(I32))
        w2_plane = sb.tile([P, N], U8, name="w2_plane", align_bytes=64)
        nc.gpsimd.memset(w2_plane[:], 0)
        load_scale_rows(w2_plane, w2_scales)

        picked_scales = sb.tile([P, S], U8, name="picked_scales", align_bytes=64)
        nc.vector.tensor_copy(picked_scales[:], x_plane[:].indirect(offs_t[:]))
        w1_low = deal_weight("w1_low", w1_raw, nc.scalar.copy, 0, pool=shared, offset=0)
        w1_q = [quantize("w1_low", w1_low[:], 2 * P)]
        w1_high = deal_weight("w1_high", w1_raw, nc.scalar.copy, 1, pool=shared, offset=0)
        pieces = [slice(0, 256), slice(256, 512), slice(512, S)]
        words = [sb.tile([P, BANK], U32, name=f"picked_words{half}", align_bytes=64) for half in range(2)]

        def pick_words(cols):
            start = cols.start % BANK
            nc.vector.tensor_copy(
                words[cols.start // BANK][:, start : start + cols.stop - cols.start],
                x_table[:].bitcast(U32).indirect(offs_t[:, cols.start // 16 : cols.stop // 16]),
            )

        h = [sb.tile([P, S], F32, name=f"h{t}") for t in range(PACK)]

        def hidden(t, cols, b):
            acc = bank(b)
            codes, scales = w1_q[t // 2]
            rows = slice(t % 2 * P, (t % 2 + 1) * P)
            width, start = cols.stop - cols.start, cols.start % BANK
            nc.tensor.matmul_mx(
                out=acc[:, :width],
                lhsT=codes[:, rows].bitcast(FP8X4),
                lhsT_scale=scales[:, rows],
                rhs=words[cols.start // BANK][:, start : start + width].bitcast(FP8X4),
                rhs_scale=picked_scales[:, cols],
                start=True,
                stop=True,
            )
            nc.scalar.activation(h[t][:, cols], acc[:, :width], SILU)

        pick_words(pieces[0])
        pick_words(pieces[1])
        w1_q.append(quantize("w1_high", w1_high[:], 2 * P))
        pick_words(pieces[2])
        for k in range(2):
            for t in range(2):
                hidden(t, pieces[k], 2 * k + t)
        for t in range(2, PACK):
            hidden(t, slice(0, BANK), 2 + t)
        for t in range(PACK):
            hidden(t, pieces[2], (6 + t) % 8)

        w3_stage = [deal_weight(f"w3_{u}", w3_raw, nc.vector.tensor_copy, u) for u in range(2)]
        w3_q = [quantize(f"w3_{u}", w3_stage[u][:], 2 * P) for u in range(2)]
        first, second, third = slice(0, 256), slice(256, 384), slice(384, V)
        rest = slice(second.start, V)

        def looked_up(d, t, cols):
            return h[t][:].indirect(pos_t[d][:, cols.start // 16 : cols.stop // 16])

        a_q = {}
        for d in range(D):
            stages = [sb.tile([P, 256, PACK], BF16, name=f"a{d}_stage{k}", align_bytes=64) for k in range(2)]
            for k, cols in enumerate((first, rest)):
                interleave(nc.vector.tensor_copy, stages[k][:], a_raw[d][:, :, cols])
            for k in range(2):
                a_q[d, k] = quantize(f"a{d}_{k}", stages[k][:].rearrange("p v j -> p (v j)"), 256)
            if d == 0:
                got_early = shared.tile([P, 3, 256], F32, name="got_early", offset=12288)
                for t in range(3):
                    nc.vector.tensor_copy(got_early[:, t, :], looked_up(0, t, first))

        def filters(d, tiles, cols, b):
            width = cols.stop - cols.start
            acc = bank(b)
            for e, t in enumerate(tiles):
                product(acc[:, e * width : (e + 1) * width], w3_q[t // 2], slice(t % 2 * P, (t % 2 + 1) * P), a_q[d, cols.start // 256], slice(cols.start % 256, cols.start % 256 + width))
            return acc[:].rearrange("p (e v) -> p e v", v=width)

        def fetch(got, d, tiles, cols, start):
            for t in tiles:
                nc.scalar.activation(got[:, t, cols.start - start : cols.stop - start], looked_up(d, t, cols), COPY)

        def multiply(terms, got, d, tiles, cols, b):
            part = slice(tiles[0], tiles[-1] + 1)
            nc.vector.tensor_tensor(terms[:, part, :], got[:, part, :], filters(d, tiles, cols, b), MULT)

        def add_terms(name, terms0, terms1):
            z = sb.tile([P, terms0.shape[2], PACK], BF16, name=name, align_bytes=64)
            nc.vector.tensor_tensor(
                z[:].rearrange("p (c i) t -> p c t i", i=4),
                terms0.rearrange("p t (c i) -> p c t i", i=4),
                terms1.rearrange("p t (c i) -> p c t i", i=4),
                ADD,
            )
            return z[:].rearrange("p v t -> p (v t)")

        def project(name, z, cols, b, copy, queue):
            width = cols.stop - cols.start
            z_q = quantize(name, z, width)
            acc = bank(b)
            product(acc[:, 0:width], (w2_codes, w2_plane), slice(0, N), z_q, slice(0, width))
            result = sb.tile([P, width], F32, name=name + "_result")
            copy(result[:], acc[:, 0:width])
            queue.dma_start(out[:, cols], result[:])

        low, high, every = [0, 1], [2, 3], [0, 1, 2, 3]
        first0 = shared.tile([P, PACK, 256], F32, name="first0", offset=4096)
        first1 = sb.tile([P, PACK, 256], F32, name="first1")
        rest0 = shared.tile([P, PACK, 256], F32, name="rest0", offset=20480)
        second1 = sb.tile([P, PACK, P], F32, name="second1")
        third1 = sb.tile([P, PACK, P], F32, name="third1")
        got_first0 = sb.tile([P, PACK, 256], F32, name="got_first0")
        got_rest0 = sb.tile([P, PACK, 256], F32, name="got_rest0")
        got_first1_low = shared.tile([P, 2, 256], F32, name="got_first1_low", offset=20480)
        got_first1 = sb.tile([P, PACK, 256], F32, name="got_first1")
        got_second1 = sb.tile([P, PACK, P], F32, name="got_second1")
        got_third1 = sb.tile([P, PACK, P], F32, name="got_third1")

        fetch(got_first0, 0, [3], first, 0)
        fetch(got_first1_low, 1, low, first, 0)
        fetch(got_first1, 1, high, first, 0)
        fetch(got_rest0, 0, every, rest, rest.start)
        fetch(got_second1, 1, every, second, second.start)
        fetch(got_third1, 1, every, third, third.start)
        multiply(first0, got_early, 0, low, first, 2)
        high_filters = filters(0, high, first, 3)
        for e, got in enumerate((got_early, got_first0)):
            nc.vector.tensor_tensor(first0[:, 2 + e, :], got[:, 2 + e, :], high_filters[:, e, :], MULT)
        multiply(first1, got_first1_low, 1, low, first, 6)
        multiply(first1, got_first1, 1, high, first, 7)
        multiply(rest0, got_rest0, 0, low, rest, 4)
        z_first = add_terms("z_first", first0[:], first1[:])
        multiply(rest0, got_rest0, 0, high, rest, 5)
        multiply(second1, got_second1, 1, every, second, 0)
        project("z_first", z_first, first, 2, nc.scalar.copy, nc.sync)
        z_second = add_terms("z_second", rest0[:, :, :P], second1[:])
        multiply(third1, got_third1, 1, every, third, 1)
        project("z_second", z_second, second, 3, nc.scalar.copy, nc.scalar)
        project("z_third", add_terms("z_third", rest0[:, :, P:], third1[:]), third, 4, nc.vector.tensor_copy, nc.sync)
